import numpy as np
import ml_dtypes


def mxq(x, axis, fmt="e4m3"):
    dtype, down = {"e4m3": (ml_dtypes.float8_e4m3fn, 7), "e5m2": (ml_dtypes.float8_e5m2, 14)}[fmt]
    v = np.moveaxis(np.asarray(x, np.float32).astype(ml_dtypes.bfloat16).astype(np.float64), axis, -1)
    blocks = v.reshape(v.shape[:-1] + (-1, 32))
    amax = np.abs(blocks).max(-1, keepdims=True)
    byte = np.maximum(np.where(amax > 0, np.frexp(amax)[1] - 1 + 127, 0) - down, 1)
    scale = np.exp2(byte - 127.0)
    codes = (blocks / scale).astype(np.float32).astype(dtype).astype(np.float64)
    return np.moveaxis((codes * scale).reshape(v.shape), -1, axis)


WIDE = False


def mx_kscale(k):
    if not WIDE:
        return np.ones(k)
    levels = np.array([10, -10, 5, -5, 0])
    if k % 512:
        return np.exp2(np.random.permutation(np.resize(levels, k // 32))).repeat(32)
    a = np.empty((k // 512, 16))
    for p in range(k // 512):
        a[p, :8] = np.random.permutation(np.resize(levels, 8))
        for g in range(8):
            far = levels[np.abs(levels - a[p, g]) >= 10]
            a[p, g + 8] = far[np.random.randint(len(far))]
    return np.exp2(a.ravel()).repeat(32)


BF16 = ml_dtypes.bfloat16


def bf(x):
    return np.asarray(x, np.float32).astype(BF16)


def f64(x):
    return np.asarray(x).astype(np.float64)


E2M1 = np.array([0.0, 0.5, 1.0, 1.5, 2.0, 3.0, 4.0, 6.0, -0.0, -0.5, -1.0, -1.5, -2.0, -3.0, -4.0, -6.0])


def pack_weight(w, fmt):
    k, n = w.shape
    w = f64(bf(w)).reshape(k // 32, 32, n)
    amax = np.abs(w).max(1)
    if fmt == "e4m3":
        byte = np.frexp(amax)[1] - 1 + 127 - 7
    else:
        mant, ex = np.frexp(amax / 6.0)
        byte = np.where(mant > 0.5, ex, ex - 1) + 127
    byte = np.clip(np.where(amax > 0, byte, 1), 1, 254)
    scaled = (w * np.exp2(127.0 - byte)[:, None, :]).reshape(k, n).astype(np.float32)
    by_word = np.ascontiguousarray(scaled.reshape(k // 512, 128, 4, n).transpose(0, 1, 3, 2))
    if fmt == "e4m3":
        words = by_word.astype(ml_dtypes.float8_e4m3fn).view(np.uint8)
    else:
        c = by_word.astype(ml_dtypes.float4_e2m1fn).view(np.uint8) & 0xF
        words = c[..., 0::2] | (c[..., 1::2] << 4)
    return np.ascontiguousarray(words), np.ascontiguousarray(byte.astype(np.uint8).reshape(k // 512, 16, n))


def unpack_weight(words, scales, fmt):
    g, p, n, _ = words.shape
    if fmt == "e4m3":
        vals = np.ascontiguousarray(words).view(ml_dtypes.float8_e4m3fn).astype(np.float64)
    else:
        nib = np.empty((g, p, n, 4), np.uint8)
        nib[..., 0::2] = words & 0xF
        nib[..., 1::2] = words >> 4
        vals = E2M1[nib]
    vals = vals * np.repeat(np.exp2(scales.astype(np.float64) - 127.0), 8, axis=1)[..., None]
    return vals.transpose(0, 1, 3, 2).reshape(g * 512, n)
def pack4(w):
    words, scales = pack_weight(w, "e2m1")
    return words.reshape(words.shape[0], 128, -1), scales


def unpack4(words, scales):
    return unpack_weight(words.reshape(words.shape[0], 128, -1, 2), scales, "e2m1")


def planes(Y):
    n, m = Y.shape
    b = f64(bf(Y)).reshape(n // 32, 32, m)
    amax = np.abs(b).max(1)
    byte = np.clip(np.where(amax > 0, np.frexp(amax)[1] - 1 + 127 - 7, 1), 1, 254)
    codes = (b * np.exp2(127.0 - byte)[:, None, :]).reshape(n, m).astype(np.float32).astype(ml_dtypes.float8_e4m3fn).view(np.uint8)
    words = codes.reshape(n // 512, 128, 4, m).transpose(0, 1, 3, 2)
    return np.ascontiguousarray(words), np.ascontiguousarray(byte.astype(np.uint8).reshape(n // 512, 16, m))


M, K, F, N = 1024, 1024, 2048, 1536

def setup_inputs():
    s = mx_kscale(K)
    t = mx_kscale(F)
    labs_t = np.random.randn(K, M) * s[:, None]
    x_words, x_scales = pack_weight(labs_t, "e4m3")
    risk = 2.5 * np.random.randn(K, F) / np.sqrt(K) / s[:, None]
    w_words, w_scales = pack4(risk)
    severity = bf(np.exp(0.3 * np.random.randn(F)) * t)
    effect = bf(1.5 * np.random.randn(F, N) / np.sqrt(F) / t[:, None])
    lower = bf(-1.0 - 0.3 * np.abs(np.random.randn(N)))
    upper = bf(1.0 + 0.3 * np.abs(np.random.randn(N)))
    unit = np.exp(0.8 * np.random.randn(N))
    worth = bf(unit)
    burden = bf(0.3 * unit * np.abs(np.random.randn(N)))
    return {"x_words": x_words, "x_scales": x_scales, "w_words": w_words, "w_scales": w_scales,
            "severity": severity, "effect": effect, "lower": lower, "upper": upper,
            "worth": worth, "burden": burden}

def reference(x_words, x_scales, w_words, w_scales, severity, effect, lower, upper, worth, burden):
    XT = unpack_weight(x_words, x_scales, "e4m3")
    W = unpack4(w_words, w_scales)
    Z = XT.T @ W
    R = 1.0 / (1.0 + np.exp(-Z))
    H = R * f64(severity)
    E = mxq(H, 1, "e4m3") @ mxq(f64(effect), 0, "e4m3")
    C = np.minimum(np.maximum(E, f64(lower)), f64(upper))
    y = C * f64(worth) - f64(burden)
    Y = y.T
    words, scales = planes(Y)
    return y, words, scales

@@ -1,0 +1,377 @@
+from contextlib import ExitStack
+
+import concourse.mybir as mybir
+from concourse.masks import make_identity
+
+M, K, F, N = 1024, 1024, 2048, 1536
+FLOPS = 2 * M * K * F + 2 * M * F * N
+
+F32 = mybir.dt.float32
+BF16 = mybir.dt.bfloat16
+I32 = mybir.dt.int32
+U32 = mybir.dt.uint32
+U8 = mybir.dt.uint8
+FP8X4 = mybir.dt.float8_e4m3fn_x4
+FP4X4 = mybir.dt.float4_e2m1fn_x4
+ACT = mybir.ActivationFunctionType
+ALU = mybir.AluOpType
+
+P = 128
+G = 512
+KP = K // G
+FP = F // G
+NG = N // G
+MH = M // G
+
+
+def tile_clipped_treatment_utility_h2_kernel(
+    tc, x_words, x_scales, w_words, w_scales, severity, effect, lower, upper, worth, burden, out_0, out_1, out_2
+):
+    nc = tc.nc
+    with ExitStack() as ctx:
+        keep = ctx.enter_context(tc.tile_pool(name="keep", bufs=1))
+        work = ctx.enter_context(tc.tile_pool(name="work", bufs=2))
+        psum = ctx.enter_context(tc.psum_pool(name="psum", bufs=7))
+        psum_sev = ctx.enter_context(tc.psum_pool(name="psum_sev", bufs=1))
+        ctx.enter_context(tc.manual_schedule())
+
+        def kept(name, shape, dtype):
+            return keep.tile(shape, dtype, name=name, align_bytes=64)
+
+        w_raw = [kept("w_raw%d" % j, [P, KP * 1024], U8) for j in range(FP)]
+        w_codes = [kept("w_codes%d" % j, [P, KP * 1024], U8) for j in range(FP)]
+        w_sraw = kept("w_sraw", [P, KP * F], U8)
+        w_sc = [kept("w_sc%d" % j, [P, KP * G], U8) for j in range(FP)]
+        x_codes = [kept("x_codes%d" % h, [P, KP * 2048], U8) for h in range(MH)]
+        x_sc = kept("x_sc", [P, KP * M], U8)
+        e_first = [kept("e_first%d" % j, [P, 4, G], BF16) for j in range(FP)]
+        e_rest = [kept("e_rest%d" % j, [P, 4, N - G], BF16) for j in range(FP)]
+        e_codes = [kept("e_codes%d" % q, [P, G], U32) for q in range(FP * NG)]
+        e_sc = [kept("e_sc%d" % q, [P, G], U8) for q in range(FP * NG)]
+        h_codes = [kept("h_codes%d" % s, [P, G], U32) for s in range(MH * FP)]
+        h_sc = [kept("h_sc%d" % s, [P, G], U8) for s in range(MH * FP)]
+        pair = [kept("pair%d" % b, [P, 4 * G], BF16) for b in range(2)]
+        y_sc = kept("y_sc", [P, NG * M], U8)
+        ident = kept("ident", [P, P], F32)
+        sev_raw = kept("sev_raw", [P, G], BF16)
+        sev_rows = kept("sev_rows", [P, 4, P], F32)
+        vec = [kept("vec%d" % v, [P, NG, 4], BF16) for v in range(4)]
+        cst = kept("cst", [P, 8, NG * 4], F32)
+        sev = psum_sev.tile([P, P, 4], F32, name="sev")
+
+        w_words32 = w_words.bitcast(I32)
+        w_scales32 = w_scales.bitcast(I32)
+        x_words32 = x_words.rearrange("g p m t -> g p (m t)").bitcast(I32)
+        x_scales32 = x_scales.bitcast(I32)
+        out_words32 = out_1.rearrange("g p m t -> g p (m t)").bitcast(I32)
+        out_scales32 = out_2.bitcast(I32)
+
+        def load_w(j):
+            nc.sync.dma_start(
+                out=w_raw[j][:].bitcast(I32).rearrange("p (g c) -> p g c", g=KP),
+                in_=w_words32[:, :, 256 * j : 256 * (j + 1)].rearrange("g p c -> p g c"),
+            )
+
+        def load_x(h):
+            nc.sync.dma_start(
+                out=x_codes[h][:].bitcast(I32).rearrange("p (g c) -> p g c", g=KP),
+                in_=x_words32[:, :, G * h : G * (h + 1)].rearrange("g p c -> p g c"),
+            )
+
+        def load_scales(plane, rows32):
+            for q in range(4):
+                nc.sync.dma_start(
+                    out=plane[32 * q : 32 * q + 4, :].bitcast(I32).rearrange("r (g c) -> r g c", g=KP),
+                    in_=rows32[:, 4 * q : 4 * q + 4, :].rearrange("g r c -> r g c"),
+                )
+
+        def load_effect(dst, j, cols):
+            rows = effect[G * j : G * (j + 1), cols].rearrange("(b t i) n -> i b t n", t=4, i=4)
+            for i in range(4):
+                nc.sync.dma_start(out=dst[i:P:4, :, :], in_=rows[i])
+
+        def permute_w(j):
+            nc.vector.tensor_copy(
+                out=w_codes[j][:].bitcast(I32).rearrange("p (g t b w) -> p g t b w", g=KP, t=4, w=2),
+                in_=w_raw[j][:].bitcast(I32).rearrange("p (g b t w) -> p g t b w", g=KP, t=4, w=2),
+            )
+            nc.vector.tensor_copy(
+                out=w_sc[j][:].bitcast(I32).rearrange("p (g t b) -> p g t b", g=KP, t=4),
+                in_=w_sraw[:].bitcast(I32).rearrange("p (g j b t) -> p j g t b", g=KP, j=FP, t=4)[:, j],
+            )
+
+        sig = {}
+
+        def stage1(s):
+            h, j = divmod(s, FP)
+            sig[s] = work.tile([P, 4, G], F32, name="sig", bufs=4)
+            for t in range(4):
+                bank = psum.tile([P, G], F32, name="bank")
+                for g in range(KP):
+                    nc.tensor.matmul_mx(
+                        out=bank[:],
+                        lhsT=w_codes[j][:, 1024 * g + 256 * t : 1024 * g + 256 * (t + 1)].bitcast(FP4X4),
+                        lhsT_scale=w_sc[j][:, G * g + P * t : G * g + P * (t + 1)],
+                        rhs=x_codes[h][:, 2048 * g : 2048 * (g + 1)].bitcast(FP8X4),
+                        rhs_scale=x_sc[:, M * g + G * h : M * g + G * (h + 1)],
+                        start=(g == 0),
+                        stop=(g == KP - 1),
+                    )
+                nc.scalar.activation(out=sig[s][:, t, :], in_=bank[:], func=ACT.Sigmoid)
+
+        def weigh(s):
+            j = s % FP
+            nc.vector.tensor_tensor(
+                out=pair[s % 2][:].rearrange("p (c i t) -> p c t i", i=2, t=4),
+                in0=sig[s][:].rearrange("p t (c i) -> p c t i", i=2),
+                in1=sev[:, j, :].unsqueeze(1).unsqueeze(3).broadcast_to([P, G // 2, 4, 2]),
+                op=ALU.mult,
+            )
+
+        def quant_h(s):
+            nc.vector.quantize_mx(out=h_codes[s][:].bitcast(FP8X4), scales=h_sc[s][:], in_=pair[s % 2][:])
+
+        def e_src(q):
+            g, j = divmod(q, FP)
+            return e_first[j][:] if g == 0 else e_rest[j][:, :, G * (g - 1) : G * g]
+
+        whole = {}
+
+        def e_whole(q, eng):
+            whole[q] = work.tile([P, 4 * G], BF16, name="grouped", align_bytes=64)
+            dst = whole[q][:].rearrange("p (u a i t) -> p a u i t", u=4, i=2, t=4)
+            src = e_src(q).rearrange("p t (a i u) -> p a u i t", i=2, u=4)
+            if eng == "V":
+                nc.vector.tensor_copy(out=dst, in_=src)
+            else:
+                nc.scalar.copy(out=dst, in_=src)
+
+        def quant_e(q, src, c0, c1):
+            nc.vector.quantize_mx(out=e_codes[q][:, c0:c1].bitcast(FP8X4), scales=e_sc[q][:, c0:c1], in_=src)
+
+        def e_pool(q, s):
+            buf = pair[(s + 1) % 2]
+            nc.gpsimd.tensor_scalar(
+                out=buf[:, 0 : 3 * G].rearrange("p (u m t) -> p u m t", u=3, t=4),
+                in0=e_src(q).rearrange("p t (m u) -> p u m t", u=4)[:, 0:3],
+                scalar1=1.0,
+                scalar2=0.0,
+                op0=ALU.mult,
+                op1=ALU.add,
+            )
+
+        last = {}
+
+        def e_last(q):
+            last[q] = work.tile([P, G], BF16, name="last", bufs=4, align_bytes=64)
+            nc.scalar.copy(
+                out=last[q][:].rearrange("p (m t) -> p m t", t=4),
+                in_=e_src(q).rearrange("p t (m u) -> p u m t", u=4)[:, 3],
+            )
+
+        def window(s, q, extra=None):
+            buf = pair[(s + 1) % 2]
+            e_pool(q, s)
+            weigh(s)
+            quant_e(q, buf[:, 0:1024], 0, 256)
+            quant_e(q, buf[:, 1024:1536], 256, 384)
+            quant_e(q, last[q][:], 384, 512)
+            if extra is not None:
+                clamp(extra[0], extra[1], range(4))
+            quant_h(s)
+
+        y_t = {}
+
+        def stage2(h, g, slots, m0=0, m1=G):
+            if (h, g) not in y_t:
+                y_t[(h, g)] = work.tile([P, 4, G], F32, name="y_t", bufs=4)
+            for t in slots:
+                bank = psum.tile([P, G], F32, name="bank")
+                for j in range(FP):
+                    q = FP * g + j
+                    nc.tensor.matmul_mx(
+                        out=bank[:, m0:m1],
+                        lhsT=e_codes[q][:, P * t : P * (t + 1)].bitcast(FP8X4),
+                        lhsT_scale=e_sc[q][:, P * t : P * (t + 1)],
+                        rhs=h_codes[FP * h + j][:, m0:m1].bitcast(FP8X4),
+                        rhs_scale=h_sc[FP * h + j][:, m0:m1],
+                        start=(j == 0),
+                        stop=(j == FP - 1),
+                    )
+                c = 4 * g + t
+                nc.scalar.activation(
+                    out=y_t[(h, g)][:, t, m0:m1], in_=bank[:, m0:m1], func=ACT.Identity,
+                    scale=cst[:, 0, c : c + 1], bias=cst[:, 1, c : c + 1],
+                )
+
+        def clamp(h, g, slots, m0=0, m1=G):
+            for t in slots:
+                c = 4 * g + t
+                nc.vector.tensor_scalar(
+                    out=y_t[(h, g)][:, t, m0:m1], in0=y_t[(h, g)][:, t, m0:m1],
+                    scalar1=cst[:, 2, c : c + 1], scalar2=cst[:, 3, c : c + 1], op0=ALU.max, op1=ALU.min,
+                )
+
+        def turn(h, g, engines, first=0):
+            for mt in range(first, first + len(engines)):
+                bank = psum.tile([P, G], F32, name="bank")
+                for t in range(4):
+                    nc.tensor.transpose(bank[:, P * t : P * (t + 1)], y_t[(h, g)][:, t, P * mt : P * (mt + 1)], ident[:])
+                rows = work.tile([P, G], F32, name="rows", bufs=4)
+                dst = rows[:].rearrange("m (p t) -> m p t", t=4)
+                src = bank[:].rearrange("m (t p) -> m p t", t=4)
+                if engines[mt - first] == "V":
+                    nc.vector.tensor_copy(out=dst, in_=src)
+                else:
+                    nc.scalar.copy(out=dst, in_=src)
+                m0 = G * h + P * mt
+                nc.sync.dma_start(out=out_0[m0 : m0 + P, G * g : G * (g + 1)], in_=rows[:])
+
+        y_b = {}
+
+        def y_group(h, g, m0=0, m1=G):
+            y_b[(h, g, m0)] = work.tile([P, 4 * G], BF16, name="grouped", align_bytes=64)
+            nc.vector.tensor_copy(
+                out=y_b[(h, g, m0)][:, 0 : 4 * (m1 - m0)].rearrange("p (c i t) -> p c t i", i=4, t=4),
+                in_=y_t[(h, g)][:, :, m0:m1].rearrange("p t (c i) -> p c t i", i=4),
+            )
+
+        def y_quant(h, g, m0=0, m1=G):
+            codes = work.tile([P, G], U32, name="y_codes", align_bytes=64)
+            c0 = G * h + m0
+            c1 = G * h + m1
+            nc.vector.quantize_mx(
+                out=codes[:, 0 : m1 - m0].bitcast(FP8X4),
+                scales=y_sc[:, M * g + c0 : M * g + c1],
+                in_=y_b[(h, g, m0)][:, 0 : 4 * (m1 - m0)],
+            )
+            nc.sync.dma_start(out=out_words32[g, :, c0:c1], in_=codes[:, 0 : m1 - m0].bitcast(I32))
+
+        def store_scales(g):
+            for q in range(4):
+                nc.sync.dma_start(
+                    out=out_scales32[g, 4 * q : 4 * q + 4, :],
+                    in_=y_sc[32 * q : 32 * q + 4, M * g : M * (g + 1)].bitcast(I32),
+                )
+
+        nc.vector.memset(w_sraw[:].bitcast(I32), 0)
+        nc.vector.memset(x_sc[:].bitcast(I32), 0)
+        nc.vector.memset(sev_rows[:], 0.0)
+        nc.gpsimd.dma_start(out=sev_raw[0:FP, :], in_=severity.rearrange("(j f) -> j f", j=FP))
+        make_identity(nc, ident[:])
+        for v, src in enumerate((lower, upper, worth, burden)):
+            nc.gpsimd.dma_start(out=vec[v][:], in_=src.rearrange("(g p t) -> p g t", g=NG, t=4))
+        load_w(0)
+        load_x(0)
+        load_scales(w_sraw, w_scales32)
+        load_scales(x_sc, x_scales32)
+        load_w(1)
+        load_effect(e_first[0], 0, slice(0, G))
+        load_w(2)
+        load_w(3)
+        load_effect(e_first[1], 1, slice(0, G))
+        load_effect(e_first[2], 2, slice(0, G))
+        load_x(1)
+        load_effect(e_first[3], 3, slice(0, G))
+        for j in range(FP):
+            load_effect(e_rest[j], j, slice(G, N))
+
+        nc.vector.tensor_copy(
+            out=sev_rows[0:FP].rearrange("j t (b i) -> j t b i", i=4),
+            in_=sev_raw[0:FP, :].rearrange("j (b t i) -> j t b i", t=4, i=4),
+        )
+        for t in range(4):
+            nc.tensor.transpose(sev[:, :, t], sev_rows[:, t, :], ident[:])
+        permute_w(0)
+        stage1(0)
+        permute_w(1)
+        stage1(1)
+
+        lo, hi, wo, bu = [vec[v][:].rearrange("p g t -> p (g t)") for v in range(4)]
+        nc.vector.tensor_copy(out=cst[:, 0, :], in_=wo)
+        nc.vector.tensor_scalar(out=cst[:, 1, :], in0=bu, scalar1=-1.0, scalar2=None, op0=ALU.mult)
+        nc.vector.tensor_tensor(out=cst[:, 4, :], in0=lo, in1=hi, op=ALU.min)
+        nc.vector.tensor_tensor(out=cst[:, 5, :], in0=hi, in1=wo, op=ALU.mult)
+        nc.vector.tensor_tensor(out=cst[:, 6, :], in0=cst[:, 4, :], in1=wo, op=ALU.mult)
+        nc.vector.tensor_tensor(out=cst[:, 7, :], in0=cst[:, 5, :], in1=bu, op=ALU.subtract)
+        nc.vector.tensor_tensor(out=cst[:, 4, :], in0=cst[:, 6, :], in1=bu, op=ALU.subtract)
+        nc.vector.tensor_tensor(out=cst[:, 2, :], in0=cst[:, 4, :], in1=cst[:, 7, :], op=ALU.min)
+        nc.vector.tensor_tensor(out=cst[:, 3, :], in0=cst[:, 4, :], in1=cst[:, 7, :], op=ALU.max)
+
+        whole[0] = pair[1]
+        nc.vector.tensor_copy(
+            out=pair[1][:].rearrange("p (u a i t) -> p a u i t", u=4, i=2, t=4),
+            in_=e_src(0).rearrange("p t (a i u) -> p a u i t", i=2, u=4),
+        )
+        permute_w(2)
+        permute_w(3)
+        quant_e(0, pair[1][:], 0, G)
+        e_last(1)
+        stage1(2)
+        window(0, 1)
+        e_last(2)
+        stage1(3)
+        window(1, 2)
+        e_last(3)
+        stage1(4)
+        window(2, 3)
+        e_last(4)
+        stage1(5)
+        window(3, 4)
+        e_last(5)
+        stage1(6)
+        e_last(6)
+        stage2(0, 0, range(4))
+        window(4, 5)
+        stage1(7)
+        e_last(7)
+        window(5, 6, (0, 0))
+        e_last(8)
+        turn(0, 0, "SSSS")
+        e_whole(9, "S")
+        window(6, 7)
+        stage2(0, 1, range(4))
+        window(7, 8)
+        stage2(1, 0, range(2))
+        clamp(0, 1, range(4))
+        e_whole(10, "V")
+        quant_e(9, whole[9][:], 0, G)
+        turn(0, 1, "SSSS")
+        stage2(1, 0, range(2, 4))
+        e_whole(11, "V")
+        quant_e(10, whole[10][:], 0, G)
+        stage2(1, 1, range(2))
+        clamp(1, 0, range(4))
+        quant_e(11, whole[11][:], 0, G)
+        turn(1, 0, "SSSS")
+        y_group(0, 0)
+        y_group(1, 0)
+        stage2(1, 1, range(2, 4))
+        y_quant(0, 0)
+        y_quant(1, 0)
+        store_scales(0)
+        stage2(0, 2, range(2))
+        clamp(1, 1, range(4))
+        turn(1, 1, "SSSS")
+        y_group(0, 1)
+        y_group(1, 1)
+        stage2(0, 2, range(2, 4))
+        y_quant(0, 1)
+        y_quant(1, 1)
+        store_scales(1)
+        half = G // 2
+        stage2(1, 2, range(4), 0, half)
+        clamp(0, 2, range(4))
+        turn(0, 2, "SSSS")
+        y_group(0, 2)
+        clamp(1, 2, range(4), 0, half)
+        y_quant(0, 2)
+        stage2(1, 2, range(4), half, G)
+        turn(1, 2, "SS")
+        y_group(1, 2, 0, half)
+        clamp(1, 2, range(4), half, G)
+        y_quant(1, 2, 0, half)
+        y_group(1, 2, half, G)
+        turn(1, 2, "SV", 2)
+        y_quant(1, 2, half, G)
+        store_scales(2)

@@ -31,8 +31,7 @@ def tile_clipped_treatment_utility_h2_kernel(
     with ExitStack() as ctx:
         keep = ctx.enter_context(tc.tile_pool(name="keep", bufs=1))
         work = ctx.enter_context(tc.tile_pool(name="work", bufs=2))
-        psum = ctx.enter_context(tc.psum_pool(name="psum", bufs=7))
-        psum_sev = ctx.enter_context(tc.psum_pool(name="psum_sev", bufs=1))
+        psum = ctx.enter_context(tc.psum_pool(name="psum", bufs=1))
         ctx.enter_context(tc.manual_schedule())
 
         def kept(name, shape, dtype):
@@ -57,7 +56,7 @@ def tile_clipped_treatment_utility_h2_kernel(
         sev_rows = kept("sev_rows", [P, 4, P], F32)
         vec = [kept("vec%d" % v, [P, NG, 4], BF16) for v in range(4)]
         cst = kept("cst", [P, 8, NG * 4], F32)
-        sev = psum_sev.tile([P, P, 4], F32, name="sev")
+        sev = kept("sev", [P, FP, 4], F32)
 
         w_words32 = w_words.bitcast(I32)
         w_scales32 = w_scales.bitcast(I32)
@@ -65,6 +64,12 @@ def tile_clipped_treatment_utility_h2_kernel(
         x_scales32 = x_scales.bitcast(I32)
         out_words32 = out_1.rearrange("g p m t -> g p (m t)").bitcast(I32)
         out_scales32 = out_2.bitcast(I32)
+
+        free_banks = ["bank%d" % b for b in range(8)]
+
+        def take_bank():
+            tag = free_banks.pop(0)
+            return tag, psum.tile([P, G], F32, name=tag)
 
         def load_w(j):
             nc.sync.dma_start(
@@ -106,7 +111,7 @@ def tile_clipped_treatment_utility_h2_kernel(
             h, j = divmod(s, FP)
             sig[s] = work.tile([P, 4, G], F32, name="sig", bufs=4)
             for t in range(4):
-                bank = psum.tile([P, G], F32, name="bank")
+                tag, bank = take_bank()
                 for g in range(KP):
                     nc.tensor.matmul_mx(
                         out=bank[:],
@@ -118,6 +123,7 @@ def tile_clipped_treatment_utility_h2_kernel(
                         stop=(g == KP - 1),
                     )
                 nc.scalar.activation(out=sig[s][:, t, :], in_=bank[:], func=ACT.Sigmoid)
+                free_banks.append(tag)
 
         def weigh(s):
             j = s % FP
@@ -138,7 +144,7 @@ def tile_clipped_treatment_utility_h2_kernel(
         whole = {}
 
         def e_whole(q, eng):
-            whole[q] = work.tile([P, 4 * G], BF16, name="grouped", align_bytes=64)
+            whole[q] = work.tile([P, 4 * G], BF16, name="grouped", bufs=3, align_bytes=64)
             dst = whole[q][:].rearrange("p (u a i t) -> p a u i t", u=4, i=2, t=4)
             src = e_src(q).rearrange("p t (a i u) -> p a u i t", i=2, u=4)
             if eng == "V":
@@ -149,36 +155,8 @@ def tile_clipped_treatment_utility_h2_kernel(
         def quant_e(q, src, c0, c1):
             nc.vector.quantize_mx(out=e_codes[q][:, c0:c1].bitcast(FP8X4), scales=e_sc[q][:, c0:c1], in_=src)
 
-        def e_pool(q, s):
-            buf = pair[(s + 1) % 2]
-            nc.gpsimd.tensor_scalar(
-                out=buf[:, 0 : 3 * G].rearrange("p (u m t) -> p u m t", u=3, t=4),
-                in0=e_src(q).rearrange("p t (m u) -> p u m t", u=4)[:, 0:3],
-                scalar1=1.0,
-                scalar2=0.0,
-                op0=ALU.mult,
-                op1=ALU.add,
-            )
-
-        last = {}
-
-        def e_last(q):
-            last[q] = work.tile([P, G], BF16, name="last", bufs=4, align_bytes=64)
-            nc.scalar.copy(
-                out=last[q][:].rearrange("p (m t) -> p m t", t=4),
-                in_=e_src(q).rearrange("p t (m u) -> p u m t", u=4)[:, 3],
-            )
-
-        def window(s, q, extra=None):
-            buf = pair[(s + 1) % 2]
-            e_pool(q, s)
-            weigh(s)
-            quant_e(q, buf[:, 0:1024], 0, 256)
-            quant_e(q, buf[:, 1024:1536], 256, 384)
-            quant_e(q, last[q][:], 384, 512)
-            if extra is not None:
-                clamp(extra[0], extra[1], range(4))
-            quant_h(s)
+        def quant_whole(q):
+            quant_e(q, whole[q][:], 0, G)
 
         y_t = {}
 
@@ -186,7 +164,7 @@ def tile_clipped_treatment_utility_h2_kernel(
             if (h, g) not in y_t:
                 y_t[(h, g)] = work.tile([P, 4, G], F32, name="y_t", bufs=4)
             for t in slots:
-                bank = psum.tile([P, G], F32, name="bank")
+                tag, bank = take_bank()
                 for j in range(FP):
                     q = FP * g + j
                     nc.tensor.matmul_mx(
@@ -203,6 +181,35 @@ def tile_clipped_treatment_utility_h2_kernel(
                     out=y_t[(h, g)][:, t, m0:m1], in_=bank[:, m0:m1], func=ACT.Identity,
                     scale=cst[:, 0, c : c + 1], bias=cst[:, 1, c : c + 1],
                 )
+                free_banks.append(tag)
+
+        held = {}
+
+        def one_pass(h, g, j):
+            if j == 0:
+                y_t[(h, g)] = work.tile([P, 4, G], F32, name="y_t", bufs=4)
+            for t in range(4):
+                if j == 0:
+                    held[(h, g, t)] = take_bank()
+                q = FP * g + j
+                nc.tensor.matmul_mx(
+                    out=held[(h, g, t)][1][:],
+                    lhsT=e_codes[q][:, P * t : P * (t + 1)].bitcast(FP8X4),
+                    lhsT_scale=e_sc[q][:, P * t : P * (t + 1)],
+                    rhs=h_codes[FP * h + j][:].bitcast(FP8X4),
+                    rhs_scale=h_sc[FP * h + j][:],
+                    start=(j == 0),
+                    stop=(j == FP - 1),
+                )
+
+        def finish(h, g):
+            for t in range(4):
+                c = 4 * g + t
+                nc.scalar.activation(
+                    out=y_t[(h, g)][:, t, :], in_=held[(h, g, t)][1][:], func=ACT.Identity,
+                    scale=cst[:, 0, c : c + 1], bias=cst[:, 1, c : c + 1],
+                )
+                free_banks.append(held[(h, g, t)][0])
 
         def clamp(h, g, slots, m0=0, m1=G):
             for t in slots:
@@ -214,7 +221,7 @@ def tile_clipped_treatment_utility_h2_kernel(
 
         def turn(h, g, engines, first=0):
             for mt in range(first, first + len(engines)):
-                bank = psum.tile([P, G], F32, name="bank")
+                tag, bank = take_bank()
                 for t in range(4):
                     nc.tensor.transpose(bank[:, P * t : P * (t + 1)], y_t[(h, g)][:, t, P * mt : P * (mt + 1)], ident[:])
                 rows = work.tile([P, G], F32, name="rows", bufs=4)
@@ -224,14 +231,16 @@ def tile_clipped_treatment_utility_h2_kernel(
                     nc.vector.tensor_copy(out=dst, in_=src)
                 else:
                     nc.scalar.copy(out=dst, in_=src)
+                free_banks.append(tag)
                 m0 = G * h + P * mt
                 nc.sync.dma_start(out=out_0[m0 : m0 + P, G * g : G * (g + 1)], in_=rows[:])
 
         y_b = {}
 
-        def y_group(h, g, m0=0, m1=G):
-            y_b[(h, g, m0)] = work.tile([P, 4 * G], BF16, name="grouped", align_bytes=64)
-            nc.vector.tensor_copy(
+        def y_group(h, g, m0=0, m1=G, eng="V"):
+            y_b[(h, g, m0)] = work.tile([P, 4 * G], BF16, name="grouped", bufs=3, align_bytes=64)
+            copy = nc.vector.tensor_copy if eng == "V" else nc.scalar.copy
+            copy(
                 out=y_b[(h, g, m0)][:, 0 : 4 * (m1 - m0)].rearrange("p (c i t) -> p c t i", i=4, t=4),
                 in_=y_t[(h, g)][:, :, m0:m1].rearrange("p t (c i) -> p c t i", i=4),
             )
@@ -259,8 +268,6 @@ def tile_clipped_treatment_utility_h2_kernel(
         nc.vector.memset(sev_rows[:], 0.0)
         nc.gpsimd.dma_start(out=sev_raw[0:FP, :], in_=severity.rearrange("(j f) -> j f", j=FP))
         make_identity(nc, ident[:])
-        for v, src in enumerate((lower, upper, worth, burden)):
-            nc.gpsimd.dma_start(out=vec[v][:], in_=src.rearrange("(g p t) -> p g t", g=NG, t=4))
         load_w(0)
         load_x(0)
         load_scales(w_sraw, w_scales32)
@@ -273,6 +280,8 @@ def tile_clipped_treatment_utility_h2_kernel(
         load_effect(e_first[2], 2, slice(0, G))
         load_x(1)
         load_effect(e_first[3], 3, slice(0, G))
+        for v, src in enumerate((lower, upper, worth, burden)):
+            nc.sync.dma_start(out=vec[v][:], in_=src.rearrange("(g p t) -> p g t", g=NG, t=4))
         for j in range(FP):
             load_effect(e_rest[j], j, slice(G, N))
 
@@ -280,13 +289,33 @@ def tile_clipped_treatment_utility_h2_kernel(
             out=sev_rows[0:FP].rearrange("j t (b i) -> j t b i", i=4),
             in_=sev_raw[0:FP, :].rearrange("j (b t i) -> j t b i", t=4, i=4),
         )
+        tag, sev_bank = take_bank()
         for t in range(4):
-            nc.tensor.transpose(sev[:, :, t], sev_rows[:, t, :], ident[:])
+            nc.tensor.transpose(sev_bank[:, P * t : P * (t + 1)], sev_rows[:, t, :], ident[:])
+        nc.vector.tensor_copy(out=sev[:], in_=sev_bank[:].rearrange("p (t j) -> p j t", t=4)[:, 0:FP, :])
+        free_banks.append(tag)
         permute_w(0)
         stage1(0)
         permute_w(1)
         stage1(1)
 
+        e_whole(0, "V")
+        permute_w(2)
+        permute_w(3)
+        stage1(2)
+        quant_whole(0)
+        weigh(0)
+        stage1(3)
+        e_whole(1, "V")
+        quant_h(0)
+        quant_whole(1)
+        weigh(1)
+        stage1(4)
+        e_whole(2, "V")
+        quant_h(1)
+        quant_whole(2)
+        e_whole(3, "S")
+        weigh(2)
         lo, hi, wo, bu = [vec[v][:].rearrange("p g t -> p (g t)") for v in range(4)]
         nc.vector.tensor_copy(out=cst[:, 0, :], in_=wo)
         nc.vector.tensor_scalar(out=cst[:, 1, :], in0=bu, scalar1=-1.0, scalar2=None, op0=ALU.mult)
@@ -298,70 +327,80 @@ def tile_clipped_treatment_utility_h2_kernel(
         nc.vector.tensor_tensor(out=cst[:, 2, :], in0=cst[:, 4, :], in1=cst[:, 7, :], op=ALU.min)
         nc.vector.tensor_tensor(out=cst[:, 3, :], in0=cst[:, 4, :], in1=cst[:, 7, :], op=ALU.max)
 
-        whole[0] = pair[1]
-        nc.vector.tensor_copy(
-            out=pair[1][:].rearrange("p (u a i t) -> p a u i t", u=4, i=2, t=4),
-            in_=e_src(0).rearrange("p t (a i u) -> p a u i t", i=2, u=4),
-        )
-        permute_w(2)
-        permute_w(3)
-        quant_e(0, pair[1][:], 0, G)
-        e_last(1)
-        stage1(2)
-        window(0, 1)
-        e_last(2)
-        stage1(3)
-        window(1, 2)
-        e_last(3)
-        stage1(4)
-        window(2, 3)
-        e_last(4)
         stage1(5)
-        window(3, 4)
-        e_last(5)
+        quant_h(2)
+        weigh(3)
         stage1(6)
-        e_last(6)
-        stage2(0, 0, range(4))
-        window(4, 5)
         stage1(7)
-        e_last(7)
-        window(5, 6, (0, 0))
-        e_last(8)
+        one_pass(0, 0, 0)
+        one_pass(0, 0, 1)
+        one_pass(0, 0, 2)
+        quant_whole(3)
+        quant_h(3)
+        one_pass(0, 0, 3)
+        e_whole(4, "V")
+        e_whole(6, "S")
+        finish(0, 0)
+        e_whole(5, "V")
+        quant_whole(4)
+        one_pass(0, 1, 0)
+        e_whole(7, "V")
+        quant_whole(5)
+        one_pass(0, 1, 1)
+        quant_whole(6)
+        one_pass(0, 1, 2)
+        quant_whole(7)
+        one_pass(0, 1, 3)
+        clamp(0, 0, range(4))
+        e_whole(8, "S")
+        finish(0, 1)
         turn(0, 0, "SSSS")
-        e_whole(9, "S")
-        window(6, 7)
-        stage2(0, 1, range(4))
-        window(7, 8)
-        stage2(1, 0, range(2))
+        weigh(4)
+        quant_whole(8)
+        quant_h(4)
+        one_pass(1, 0, 0)
+        y_group(0, 0, eng="S")
+        weigh(5)
         clamp(0, 1, range(4))
-        e_whole(10, "V")
-        quant_e(9, whole[9][:], 0, G)
+        quant_h(5)
         turn(0, 1, "SSSS")
-        stage2(1, 0, range(2, 4))
-        e_whole(11, "V")
-        quant_e(10, whole[10][:], 0, G)
-        stage2(1, 1, range(2))
-        clamp(1, 0, range(4))
-        quant_e(11, whole[11][:], 0, G)
-        turn(1, 0, "SSSS")
-        y_group(0, 0)
-        y_group(1, 0)
-        stage2(1, 1, range(2, 4))
+        one_pass(1, 0, 1)
+        e_whole(9, "S")
+        weigh(6)
         y_quant(0, 0)
+        quant_h(6)
+        one_pass(1, 0, 2)
+        one_pass(1, 1, 0)
+        one_pass(1, 1, 1)
+        one_pass(1, 1, 2)
+        e_whole(10, "S")
+        weigh(7)
+        quant_whole(9)
+        quant_h(7)
+        one_pass(1, 0, 3)
+        finish(1, 0)
+        one_pass(1, 1, 3)
+        e_whole(11, "V")
+        quant_whole(10)
+        clamp(1, 0, range(4))
+        quant_whole(11)
+        finish(1, 1)
+        stage2(0, 2, range(2))
+        turn(1, 0, "SSSS")
+        y_group(0, 1)
+        clamp(1, 1, range(4))
+        y_group(1, 0)
+        y_quant(0, 1)
+        stage2(0, 2, range(2, 4))
+        turn(1, 1, "SSSS")
         y_quant(1, 0)
         store_scales(0)
-        stage2(0, 2, range(2))
-        clamp(1, 1, range(4))
-        turn(1, 1, "SSSS")
-        y_group(0, 1)
         y_group(1, 1)
-        stage2(0, 2, range(2, 4))
-        y_quant(0, 1)
+        clamp(0, 2, range(4))
         y_quant(1, 1)
         store_scales(1)
         half = G // 2
         stage2(1, 2, range(4), 0, half)
-        clamp(0, 2, range(4))
         turn(0, 2, "SSSS")
         y_group(0, 2)
         clamp(1, 2, range(4), 0, half)

@@ -39,10 +39,10 @@ def tile_clipped_treatment_utility_h2_kernel(
 
         w_raw = [kept("w_raw%d" % j, [P, KP * 1024], U8) for j in range(FP)]
         w_codes = [kept("w_codes%d" % j, [P, KP * 1024], U8) for j in range(FP)]
-        w_sraw = kept("w_sraw", [P, KP * F], U8)
+        w_sraw = [kept("w_sraw%d" % a, [P, KP * F // 2], U8) for a in range(2)]
         w_sc = [kept("w_sc%d" % j, [P, KP * G], U8) for j in range(FP)]
         x_codes = [kept("x_codes%d" % h, [P, KP * 2048], U8) for h in range(MH)]
-        x_sc = kept("x_sc", [P, KP * M], U8)
+        x_sc = [kept("x_sc%d" % h, [P, KP * G], U8) for h in range(MH)]
         e_first = [kept("e_first%d" % j, [P, 4, G], BF16) for j in range(FP)]
         e_rest = [kept("e_rest%d" % j, [P, 4, N - G], BF16) for j in range(FP)]
         e_codes = [kept("e_codes%d" % q, [P, G], U32) for q in range(FP * NG)]
@@ -83,11 +83,12 @@ def tile_clipped_treatment_utility_h2_kernel(
                 in_=x_words32[:, :, G * h : G * (h + 1)].rearrange("g p c -> p g c"),
             )
 
-        def load_scales(plane, rows32):
+        def load_scales(plane, rows32, half):
+            width = rows32.shape[2] // 2
             for q in range(4):
                 nc.sync.dma_start(
                     out=plane[32 * q : 32 * q + 4, :].bitcast(I32).rearrange("r (g c) -> r g c", g=KP),
-                    in_=rows32[:, 4 * q : 4 * q + 4, :].rearrange("g r c -> r g c"),
+                    in_=rows32[:, 4 * q : 4 * q + 4, width * half : width * (half + 1)].rearrange("g r c -> r g c"),
                 )
 
         def load_effect(dst, j, cols):
@@ -102,7 +103,7 @@ def tile_clipped_treatment_utility_h2_kernel(
             )
             nc.vector.tensor_copy(
                 out=w_sc[j][:].bitcast(I32).rearrange("p (g t b) -> p g t b", g=KP, t=4),
-                in_=w_sraw[:].bitcast(I32).rearrange("p (g j b t) -> p j g t b", g=KP, j=FP, t=4)[:, j],
+                in_=w_sraw[j // 2][:].bitcast(I32).rearrange("p (g j b t) -> p j g t b", g=KP, j=2, t=4)[:, j % 2],
             )
 
         sig = {}
@@ -118,7 +119,7 @@ def tile_clipped_treatment_utility_h2_kernel(
                         lhsT=w_codes[j][:, 1024 * g + 256 * t : 1024 * g + 256 * (t + 1)].bitcast(FP4X4),
                         lhsT_scale=w_sc[j][:, G * g + P * t : G * g + P * (t + 1)],
                         rhs=x_codes[h][:, 2048 * g : 2048 * (g + 1)].bitcast(FP8X4),
-                        rhs_scale=x_sc[:, M * g + G * h : M * g + G * (h + 1)],
+                        rhs_scale=x_sc[h][:, G * g : G * (g + 1)],
                         start=(g == 0),
                         stop=(g == KP - 1),
                     )
@@ -263,59 +264,64 @@ def tile_clipped_treatment_utility_h2_kernel(
                     in_=y_sc[32 * q : 32 * q + 4, M * g : M * (g + 1)].bitcast(I32),
                 )
 
-        nc.vector.memset(w_sraw[:].bitcast(I32), 0)
-        nc.vector.memset(x_sc[:].bitcast(I32), 0)
+        nc.vector.memset(w_sraw[0][:].bitcast(I32), 0)
+        nc.vector.memset(x_sc[0][:].bitcast(I32), 0)
         nc.vector.memset(sev_rows[:], 0.0)
+        nc.vector.memset(w_sraw[1][:].bitcast(I32), 0)
+        nc.vector.memset(x_sc[1][:].bitcast(I32), 0)
         nc.gpsimd.dma_start(out=sev_raw[0:FP, :], in_=severity.rearrange("(j f) -> j f", j=FP))
         make_identity(nc, ident[:])
         load_w(0)
+        load_scales(w_sraw[0], w_scales32, 0)
         load_x(0)
-        load_scales(w_sraw, w_scales32)
-        load_scales(x_sc, x_scales32)
+        load_scales(x_sc[0], x_scales32, 0)
         load_w(1)
         load_effect(e_first[0], 0, slice(0, G))
         load_w(2)
+        load_scales(w_sraw[1], w_scales32, 1)
         load_w(3)
         load_effect(e_first[1], 1, slice(0, G))
         load_effect(e_first[2], 2, slice(0, G))
         load_x(1)
+        load_scales(x_sc[1], x_scales32, 1)
         load_effect(e_first[3], 3, slice(0, G))
         for v, src in enumerate((lower, upper, worth, burden)):
             nc.sync.dma_start(out=vec[v][:], in_=src.rearrange("(g p t) -> p g t", g=NG, t=4))
         for j in range(FP):
             load_effect(e_rest[j], j, slice(G, N))
 
+        permute_w(0)
         nc.vector.tensor_copy(
             out=sev_rows[0:FP].rearrange("j t (b i) -> j t b i", i=4),
             in_=sev_raw[0:FP, :].rearrange("j (b t i) -> j t b i", t=4, i=4),
         )
+        stage1(0)
+        permute_w(1)
         tag, sev_bank = take_bank()
         for t in range(4):
             nc.tensor.transpose(sev_bank[:, P * t : P * (t + 1)], sev_rows[:, t, :], ident[:])
+        stage1(1)
+        e_whole(0, "V")
         nc.vector.tensor_copy(out=sev[:], in_=sev_bank[:].rearrange("p (t j) -> p j t", t=4)[:, 0:FP, :])
         free_banks.append(tag)
-        permute_w(0)
-        stage1(0)
-        permute_w(1)
-        stage1(1)
-
-        e_whole(0, "V")
         permute_w(2)
-        permute_w(3)
         stage1(2)
-        quant_whole(0)
         weigh(0)
+        permute_w(3)
         stage1(3)
-        e_whole(1, "V")
+        quant_whole(0)
         quant_h(0)
-        quant_whole(1)
+        e_whole(1, "V")
         weigh(1)
+        quant_whole(1)
         stage1(4)
-        e_whole(2, "V")
         quant_h(1)
-        quant_whole(2)
+        e_whole(2, "V")
         e_whole(3, "S")
         weigh(2)
+        quant_whole(2)
+        stage1(5)
+        quant_h(2)
         lo, hi, wo, bu = [vec[v][:].rearrange("p g t -> p (g t)") for v in range(4)]
         nc.vector.tensor_copy(out=cst[:, 0, :], in_=wo)
         nc.vector.tensor_scalar(out=cst[:, 1, :], in0=bu, scalar1=-1.0, scalar2=None, op0=ALU.mult)
@@ -327,8 +333,6 @@ def tile_clipped_treatment_utility_h2_kernel(
         nc.vector.tensor_tensor(out=cst[:, 2, :], in0=cst[:, 4, :], in1=cst[:, 7, :], op=ALU.min)
         nc.vector.tensor_tensor(out=cst[:, 3, :], in0=cst[:, 4, :], in1=cst[:, 7, :], op=ALU.max)
 
-        stage1(5)
-        quant_h(2)
         weigh(3)
         stage1(6)
         stage1(7)
@@ -382,8 +386,8 @@ def tile_clipped_treatment_utility_h2_kernel(
         one_pass(1, 1, 3)
         e_whole(11, "V")
         quant_whole(10)
-        clamp(1, 0, range(4))
         quant_whole(11)
+        clamp(1, 0, range(4))
         finish(1, 1)
         stage2(0, 2, range(2))
         turn(1, 0, "SSSS")

@@ -17,11 +17,22 @@ ACT = mybir.ActivationFunctionType
 ALU = mybir.AluOpType
 
 P = 128
-G = 512
-KP = K // G
-FP = F // G
-NG = N // G
-MH = M // G
+SLOTS = 4
+GROUP = P * SLOTS
+LAB_GROUPS = K // GROUP
+RISK_GROUPS = F // GROUP
+PAIR_GROUPS = N // GROUP
+HALVES = M // GROUP
+BANKS = 8
+QUADRANT = 32
+RUN = 4
+W_BYTES = 2 * GROUP
+X_BYTES = 4 * GROUP
+
+SMALL_SLOTS = 13
+LARGE_SLOTS = 8
+SIGMOID_SLOTS = 4
+BLOCK_SLOTS = 4
 
 
 def tile_clipped_treatment_utility_h2_kernel(
@@ -30,391 +41,417 @@ def tile_clipped_treatment_utility_h2_kernel(
     nc = tc.nc
     with ExitStack() as ctx:
         keep = ctx.enter_context(tc.tile_pool(name="keep", bufs=1))
-        work = ctx.enter_context(tc.tile_pool(name="work", bufs=2))
+        work = ctx.enter_context(tc.tile_pool(name="work", bufs=1))
         psum = ctx.enter_context(tc.psum_pool(name="psum", bufs=1))
         ctx.enter_context(tc.manual_schedule())
 
         def kept(name, shape, dtype):
             return keep.tile(shape, dtype, name=name, align_bytes=64)
 
-        w_raw = [kept("w_raw%d" % j, [P, KP * 1024], U8) for j in range(FP)]
-        w_codes = [kept("w_codes%d" % j, [P, KP * 1024], U8) for j in range(FP)]
-        w_sraw = [kept("w_sraw%d" % a, [P, KP * F // 2], U8) for a in range(2)]
-        w_sc = [kept("w_sc%d" % j, [P, KP * G], U8) for j in range(FP)]
-        x_codes = [kept("x_codes%d" % h, [P, KP * 2048], U8) for h in range(MH)]
-        x_sc = [kept("x_sc%d" % h, [P, KP * G], U8) for h in range(MH)]
-        e_first = [kept("e_first%d" % j, [P, 4, G], BF16) for j in range(FP)]
-        e_rest = [kept("e_rest%d" % j, [P, 4, N - G], BF16) for j in range(FP)]
-        e_codes = [kept("e_codes%d" % q, [P, G], U32) for q in range(FP * NG)]
-        e_sc = [kept("e_sc%d" % q, [P, G], U8) for q in range(FP * NG)]
-        h_codes = [kept("h_codes%d" % s, [P, G], U32) for s in range(MH * FP)]
-        h_sc = [kept("h_sc%d" % s, [P, G], U8) for s in range(MH * FP)]
-        pair = [kept("pair%d" % b, [P, 4 * G], BF16) for b in range(2)]
-        y_sc = kept("y_sc", [P, NG * M], U8)
+        def small(name, shape, dtype):
+            return work.tile(shape, dtype, name=name, tag="small", bufs=SMALL_SLOTS, align_bytes=64)
+
+        def large(name, shape, dtype):
+            return work.tile(shape, dtype, name=name, tag="large", bufs=LARGE_SLOTS, align_bytes=64)
+
+        risk_groups = range(RISK_GROUPS)
+        pieces = [(j, g) for g in range(PAIR_GROUPS) for j in risk_groups]
+        h_parts = [(h, j) for h in range(HALVES) for j in risk_groups]
+
+        w_raw = [small("w_raw", [P, LAB_GROUPS * W_BYTES], U8) for j in risk_groups]
+        w_codes = [kept("w_codes%d" % j, [P, LAB_GROUPS * W_BYTES], U8) for j in risk_groups]
+        w_scale_raw = [kept("w_scale_raw%d" % a, [P, LAB_GROUPS * F // 2], U8) for a in range(2)]
+        w_scale = [kept("w_scale%d" % j, [P, LAB_GROUPS * GROUP], U8) for j in risk_groups]
+        x_scale = [kept("x_scale%d" % h, [P, LAB_GROUPS * GROUP], U8) for h in range(HALVES)]
+        effect_first = [large("effect_first", [P, SLOTS, GROUP], BF16) for j in risk_groups]
+        x_codes = [large("x_codes", [P, LAB_GROUPS * X_BYTES], U8) for h in range(HALVES)]
+        effect_rest = [kept("effect_rest%d" % j, [P, SLOTS, N - GROUP], BF16) for j in risk_groups]
+        e_codes = {(j, g): kept("e_codes%d_%d" % (j, g), [P, GROUP], U32) for j, g in pieces}
+        e_scale = {(j, g): kept("e_scale%d_%d" % (j, g), [P, GROUP], U8) for j, g in pieces}
+        h_codes = {(h, j): kept("h_codes%d_%d" % (h, j), [P, GROUP], U32) for h, j in h_parts}
+        h_scale = {(h, j): kept("h_scale%d_%d" % (h, j), [P, GROUP], U8) for h, j in h_parts}
+        h_grouped = [kept("h_grouped%d" % b, [P, SLOTS * GROUP], BF16) for b in range(2)]
+        y_scale = kept("y_scale", [P, PAIR_GROUPS * M], U8)
         ident = kept("ident", [P, P], F32)
-        sev_raw = kept("sev_raw", [P, G], BF16)
-        sev_rows = kept("sev_rows", [P, 4, P], F32)
-        vec = [kept("vec%d" % v, [P, NG, 4], BF16) for v in range(4)]
-        cst = kept("cst", [P, 8, NG * 4], F32)
-        sev = kept("sev", [P, FP, 4], F32)
+        severity_raw = kept("severity_raw", [P, GROUP], BF16)
+        severity_rows = small("severity_rows", [P, SLOTS, P], F32)
+        severity_col = kept("severity_col", [P, RISK_GROUPS, SLOTS], F32)
+        pair_cols = PAIR_GROUPS * SLOTS
+        pair_in = [kept("pair_in%d" % v, [P, pair_cols], BF16) for v in range(4)]
+        gain, shift, low, high, least, image_least, image_upper = [
+            kept(name, [P, pair_cols], F32)
+            for name in ("gain", "shift", "low", "high", "least", "image_least", "image_upper")
+        ]
 
         w_words32 = w_words.bitcast(I32)
         w_scales32 = w_scales.bitcast(I32)
-        x_words32 = x_words.rearrange("g p m t -> g p (m t)").bitcast(I32)
+        x_words32 = x_words.rearrange("c p m t -> c p (m t)").bitcast(I32)
         x_scales32 = x_scales.bitcast(I32)
         out_words32 = out_1.rearrange("g p m t -> g p (m t)").bitcast(I32)
         out_scales32 = out_2.bitcast(I32)
 
-        free_banks = ["bank%d" % b for b in range(8)]
+        free_banks = ["bank%d" % b for b in range(BANKS)]
 
         def take_bank():
             tag = free_banks.pop(0)
-            return tag, psum.tile([P, G], F32, name=tag)
+            return tag, psum.tile([P, GROUP], F32, name=tag)
 
         def load_w(j):
+            words = W_BYTES // 4
             nc.sync.dma_start(
-                out=w_raw[j][:].bitcast(I32).rearrange("p (g c) -> p g c", g=KP),
-                in_=w_words32[:, :, 256 * j : 256 * (j + 1)].rearrange("g p c -> p g c"),
+                out=w_raw[j][:].bitcast(I32).rearrange("p (c w) -> p c w", c=LAB_GROUPS),
+                in_=w_words32[:, :, words * j : words * (j + 1)].rearrange("c p w -> p c w"),
             )
 
         def load_x(h):
             nc.sync.dma_start(
-                out=x_codes[h][:].bitcast(I32).rearrange("p (g c) -> p g c", g=KP),
-                in_=x_words32[:, :, G * h : G * (h + 1)].rearrange("g p c -> p g c"),
+                out=x_codes[h][:].bitcast(I32).rearrange("p (c w) -> p c w", c=LAB_GROUPS),
+                in_=x_words32[:, :, GROUP * h : GROUP * (h + 1)].rearrange("c p w -> p c w"),
             )
 
-        def load_scales(plane, rows32, half):
-            width = rows32.shape[2] // 2
+        def load_scales(queue, plane, rows32, half):
+            words = rows32.shape[2] // 2
             for q in range(4):
-                nc.sync.dma_start(
-                    out=plane[32 * q : 32 * q + 4, :].bitcast(I32).rearrange("r (g c) -> r g c", g=KP),
-                    in_=rows32[:, 4 * q : 4 * q + 4, width * half : width * (half + 1)].rearrange("g r c -> r g c"),
+                queue.dma_start(
+                    out=plane[QUADRANT * q : QUADRANT * q + 4, :].bitcast(I32).rearrange("r (c w) -> r c w", c=LAB_GROUPS),
+                    in_=rows32[:, 4 * q : 4 * q + 4, words * half : words * (half + 1)].rearrange("c r w -> r c w"),
                 )
 
         def load_effect(dst, j, cols):
-            rows = effect[G * j : G * (j + 1), cols].rearrange("(b t i) n -> i b t n", t=4, i=4)
-            for i in range(4):
-                nc.sync.dma_start(out=dst[i:P:4, :, :], in_=rows[i])
+            rows = effect[GROUP * j : GROUP * (j + 1), cols].rearrange("(b t i) n -> i b t n", t=SLOTS, i=RUN)
+            for i in range(RUN):
+                nc.sync.dma_start(out=dst[i:P:RUN, :, :], in_=rows[i])
 
-        def permute_w(j):
+        def order_w(j):
             nc.vector.tensor_copy(
-                out=w_codes[j][:].bitcast(I32).rearrange("p (g t b w) -> p g t b w", g=KP, t=4, w=2),
-                in_=w_raw[j][:].bitcast(I32).rearrange("p (g b t w) -> p g t b w", g=KP, t=4, w=2),
+                out=w_codes[j][:].bitcast(I32).rearrange("p (c t b w) -> p c t b w", c=LAB_GROUPS, t=SLOTS, w=2),
+                in_=w_raw[j][:].bitcast(I32).rearrange("p (c b t w) -> p c t b w", c=LAB_GROUPS, t=SLOTS, w=2),
             )
+            raw = w_scale_raw[j // 2][:].bitcast(I32)
             nc.vector.tensor_copy(
-                out=w_sc[j][:].bitcast(I32).rearrange("p (g t b) -> p g t b", g=KP, t=4),
-                in_=w_sraw[j // 2][:].bitcast(I32).rearrange("p (g j b t) -> p j g t b", g=KP, j=2, t=4)[:, j % 2],
+                out=w_scale[j][:].bitcast(I32).rearrange("p (c t b) -> p c t b", c=LAB_GROUPS, t=SLOTS),
+                in_=raw.rearrange("p (c j b t) -> p j c t b", c=LAB_GROUPS, j=2, t=SLOTS)[:, j % 2],
             )
 
-        sig = {}
+        scores = {}
 
-        def stage1(s):
-            h, j = divmod(s, FP)
-            sig[s] = work.tile([P, 4, G], F32, name="sig", bufs=4)
-            for t in range(4):
+        def risk_scores(h, j):
+            scores[h, j] = work.tile([P, SLOTS, GROUP], F32, name="scores", bufs=SIGMOID_SLOTS)
+            for t in range(SLOTS):
                 tag, bank = take_bank()
-                for g in range(KP):
+                for c in range(LAB_GROUPS):
+                    col = GROUP * c + P * t
                     nc.tensor.matmul_mx(
                         out=bank[:],
-                        lhsT=w_codes[j][:, 1024 * g + 256 * t : 1024 * g + 256 * (t + 1)].bitcast(FP4X4),
-                        lhsT_scale=w_sc[j][:, G * g + P * t : G * g + P * (t + 1)],
-                        rhs=x_codes[h][:, 2048 * g : 2048 * (g + 1)].bitcast(FP8X4),
-                        rhs_scale=x_sc[h][:, G * g : G * (g + 1)],
-                        start=(g == 0),
-                        stop=(g == KP - 1),
+                        lhsT=w_codes[j][:, 2 * col : 2 * (col + P)].bitcast(FP4X4),
+                        lhsT_scale=w_scale[j][:, col : col + P],
+                        rhs=x_codes[h][:, X_BYTES * c : X_BYTES * (c + 1)].bitcast(FP8X4),
+                        rhs_scale=x_scale[h][:, GROUP * c : GROUP * (c + 1)],
+                        start=(c == 0),
+                        stop=(c == LAB_GROUPS - 1),
                     )
-                nc.scalar.activation(out=sig[s][:, t, :], in_=bank[:], func=ACT.Sigmoid)
+                nc.scalar.activation(out=scores[h, j][:, t, :], in_=bank[:], func=ACT.Sigmoid)
                 free_banks.append(tag)
 
-        def weigh(s):
-            j = s % FP
+        def weigh(h, j):
             nc.vector.tensor_tensor(
-                out=pair[s % 2][:].rearrange("p (c i t) -> p c t i", i=2, t=4),
-                in0=sig[s][:].rearrange("p t (c i) -> p c t i", i=2),
-                in1=sev[:, j, :].unsqueeze(1).unsqueeze(3).broadcast_to([P, G // 2, 4, 2]),
+                out=h_grouped[j % 2][:].rearrange("p (a i t) -> p a t i", i=2, t=SLOTS),
+                in0=scores[h, j][:].rearrange("p t (a i) -> p a t i", i=2),
+                in1=severity_col[:, j, :].unsqueeze(1).unsqueeze(3).broadcast_to([P, GROUP // 2, SLOTS, 2]),
                 op=ALU.mult,
             )
 
-        def quant_h(s):
-            nc.vector.quantize_mx(out=h_codes[s][:].bitcast(FP8X4), scales=h_sc[s][:], in_=pair[s % 2][:])
+        def quantise_h(h, j):
+            nc.vector.quantize_mx(out=h_codes[h, j][:].bitcast(FP8X4), scales=h_scale[h, j][:], in_=h_grouped[j % 2][:])
 
-        def e_src(q):
-            g, j = divmod(q, FP)
-            return e_first[j][:] if g == 0 else e_rest[j][:, :, G * (g - 1) : G * g]
+        e_grouped = {}
 
-        whole = {}
+        def group_effect(j, g, move):
+            raw = effect_first[j][:] if g == 0 else effect_rest[j][:, :, GROUP * (g - 1) : GROUP * g]
+            e_grouped[j, g] = large("grouped", [P, SLOTS * GROUP], BF16)
+            move(
+                out=e_grouped[j, g][:].rearrange("p (u a i t) -> p a u i t", u=SLOTS, i=2, t=SLOTS),
+                in_=raw.rearrange("p t (a i u) -> p a u i t", i=2, u=SLOTS),
+            )
 
-        def e_whole(q, eng):
-            whole[q] = work.tile([P, 4 * G], BF16, name="grouped", bufs=3, align_bytes=64)
-            dst = whole[q][:].rearrange("p (u a i t) -> p a u i t", u=4, i=2, t=4)
-            src = e_src(q).rearrange("p t (a i u) -> p a u i t", i=2, u=4)
-            if eng == "V":
-                nc.vector.tensor_copy(out=dst, in_=src)
-            else:
-                nc.scalar.copy(out=dst, in_=src)
-
-        def quant_e(q, src, c0, c1):
-            nc.vector.quantize_mx(out=e_codes[q][:, c0:c1].bitcast(FP8X4), scales=e_sc[q][:, c0:c1], in_=src)
-
-        def quant_whole(q):
-            quant_e(q, whole[q][:], 0, G)
+        def quantise_effect(j, g):
+            nc.vector.quantize_mx(out=e_codes[j, g][:].bitcast(FP8X4), scales=e_scale[j, g][:], in_=e_grouped[j, g][:])
 
         y_t = {}
 
-        def stage2(h, g, slots, m0=0, m1=G):
-            if (h, g) not in y_t:
-                y_t[(h, g)] = work.tile([P, 4, G], F32, name="y_t", bufs=4)
-            for t in slots:
-                tag, bank = take_bank()
-                for j in range(FP):
-                    q = FP * g + j
-                    nc.tensor.matmul_mx(
-                        out=bank[:, m0:m1],
-                        lhsT=e_codes[q][:, P * t : P * (t + 1)].bitcast(FP8X4),
-                        lhsT_scale=e_sc[q][:, P * t : P * (t + 1)],
-                        rhs=h_codes[FP * h + j][:, m0:m1].bitcast(FP8X4),
-                        rhs_scale=h_sc[FP * h + j][:, m0:m1],
-                        start=(j == 0),
-                        stop=(j == FP - 1),
-                    )
-                c = 4 * g + t
-                nc.scalar.activation(
-                    out=y_t[(h, g)][:, t, m0:m1], in_=bank[:, m0:m1], func=ACT.Identity,
-                    scale=cst[:, 0, c : c + 1], bias=cst[:, 1, c : c + 1],
-                )
-                free_banks.append(tag)
+        def new_block(h, g):
+            y_t[h, g] = work.tile([P, SLOTS, GROUP], F32, name="y_t", bufs=BLOCK_SLOTS)
 
-        held = {}
+        def effect_pass(bank, h, g, t, j, cols):
+            nc.tensor.matmul_mx(
+                out=bank[:, cols],
+                lhsT=e_codes[j, g][:, P * t : P * (t + 1)].bitcast(FP8X4),
+                lhsT_scale=e_scale[j, g][:, P * t : P * (t + 1)],
+                rhs=h_codes[h, j][:, cols].bitcast(FP8X4),
+                rhs_scale=h_scale[h, j][:, cols],
+                start=(j == 0),
+                stop=(j == RISK_GROUPS - 1),
+            )
 
-        def one_pass(h, g, j):
+        def empty_bank(tag, bank, h, g, t, cols):
+            col = SLOTS * g + t
+            nc.scalar.activation(
+                out=y_t[h, g][:, t, cols],
+                in_=bank[:, cols],
+                func=ACT.Identity,
+                scale=gain[:, col : col + 1],
+                bias=shift[:, col : col + 1],
+            )
+            free_banks.append(tag)
+
+        whole = slice(0, GROUP)
+        open_banks = {}
+
+        def block_pass(h, g, j):
             if j == 0:
-                y_t[(h, g)] = work.tile([P, 4, G], F32, name="y_t", bufs=4)
-            for t in range(4):
+                new_block(h, g)
+            for t in range(SLOTS):
                 if j == 0:
-                    held[(h, g, t)] = take_bank()
-                q = FP * g + j
-                nc.tensor.matmul_mx(
-                    out=held[(h, g, t)][1][:],
-                    lhsT=e_codes[q][:, P * t : P * (t + 1)].bitcast(FP8X4),
-                    lhsT_scale=e_sc[q][:, P * t : P * (t + 1)],
-                    rhs=h_codes[FP * h + j][:].bitcast(FP8X4),
-                    rhs_scale=h_sc[FP * h + j][:],
-                    start=(j == 0),
-                    stop=(j == FP - 1),
-                )
+                    open_banks[h, g, t] = take_bank()
+                effect_pass(open_banks[h, g, t][1], h, g, t, j, whole)
 
-        def finish(h, g):
-            for t in range(4):
-                c = 4 * g + t
-                nc.scalar.activation(
-                    out=y_t[(h, g)][:, t, :], in_=held[(h, g, t)][1][:], func=ACT.Identity,
-                    scale=cst[:, 0, c : c + 1], bias=cst[:, 1, c : c + 1],
-                )
-                free_banks.append(held[(h, g, t)][0])
+        def close_block(h, g):
+            for t in range(SLOTS):
+                empty_bank(*open_banks[h, g, t], h, g, t, whole)
 
-        def clamp(h, g, slots, m0=0, m1=G):
+        def block_slots(h, g, slots, cols):
             for t in slots:
-                c = 4 * g + t
+                tag, bank = take_bank()
+                for j in risk_groups:
+                    effect_pass(bank, h, g, t, j, cols)
+                empty_bank(tag, bank, h, g, t, cols)
+
+        def bound(h, g, cols):
+            for t in range(SLOTS):
+                col = SLOTS * g + t
                 nc.vector.tensor_scalar(
-                    out=y_t[(h, g)][:, t, m0:m1], in0=y_t[(h, g)][:, t, m0:m1],
-                    scalar1=cst[:, 2, c : c + 1], scalar2=cst[:, 3, c : c + 1], op0=ALU.max, op1=ALU.min,
+                    out=y_t[h, g][:, t, cols],
+                    in0=y_t[h, g][:, t, cols],
+                    scalar1=low[:, col : col + 1],
+                    scalar2=high[:, col : col + 1],
+                    op0=ALU.max,
+                    op1=ALU.min,
                 )
 
-        def turn(h, g, engines, first=0):
-            for mt in range(first, first + len(engines)):
-                tag, bank = take_bank()
-                for t in range(4):
-                    nc.tensor.transpose(bank[:, P * t : P * (t + 1)], y_t[(h, g)][:, t, P * mt : P * (mt + 1)], ident[:])
-                rows = work.tile([P, G], F32, name="rows", bufs=4)
-                dst = rows[:].rearrange("m (p t) -> m p t", t=4)
-                src = bank[:].rearrange("m (t p) -> m p t", t=4)
-                if engines[mt - first] == "V":
-                    nc.vector.tensor_copy(out=dst, in_=src)
-                else:
-                    nc.scalar.copy(out=dst, in_=src)
-                free_banks.append(tag)
-                m0 = G * h + P * mt
-                nc.sync.dma_start(out=out_0[m0 : m0 + P, G * g : G * (g + 1)], in_=rows[:])
+        def store_rows(h, g, tile_index, move):
+            tag, bank = take_bank()
+            first = P * tile_index
+            for t in range(SLOTS):
+                nc.tensor.transpose(bank[:, P * t : P * (t + 1)], y_t[h, g][:, t, first : first + P], ident[:])
+            rows = small("rows", [P, GROUP], F32)
+            move(
+                out=rows[:].rearrange("m (p t) -> m p t", t=SLOTS),
+                in_=bank[:].rearrange("m (t p) -> m p t", t=SLOTS),
+            )
+            free_banks.append(tag)
+            row = GROUP * h + first
+            nc.sync.dma_start(out=out_0[row : row + P, GROUP * g : GROUP * (g + 1)], in_=rows[:])
 
-        y_b = {}
+        def store_block(h, g):
+            for tile_index in range(GROUP // P):
+                store_rows(h, g, tile_index, on_scalar)
 
-        def y_group(h, g, m0=0, m1=G, eng="V"):
-            y_b[(h, g, m0)] = work.tile([P, 4 * G], BF16, name="grouped", bufs=3, align_bytes=64)
-            copy = nc.vector.tensor_copy if eng == "V" else nc.scalar.copy
-            copy(
-                out=y_b[(h, g, m0)][:, 0 : 4 * (m1 - m0)].rearrange("p (c i t) -> p c t i", i=4, t=4),
-                in_=y_t[(h, g)][:, :, m0:m1].rearrange("p t (c i) -> p c t i", i=4),
+        y_grouped = {}
+
+        def group_y(h, g, cols, move):
+            width = SLOTS * (cols.stop - cols.start)
+            staged = large("grouped", [P, SLOTS * GROUP], BF16)
+            y_grouped[h, g, cols.start] = staged[:, 0:width]
+            move(
+                out=staged[:, 0:width].rearrange("p (a i t) -> p a t i", i=4, t=SLOTS),
+                in_=y_t[h, g][:, :, cols].rearrange("p t (a i) -> p a t i", i=4),
             )
 
-        def y_quant(h, g, m0=0, m1=G):
-            codes = work.tile([P, G], U32, name="y_codes", align_bytes=64)
-            c0 = G * h + m0
-            c1 = G * h + m1
+        def quantise_y(h, g, cols):
+            codes = small("y_codes", [P, GROUP], U32)[:, 0 : cols.stop - cols.start]
+            first = GROUP * h + cols.start
+            last = GROUP * h + cols.stop
             nc.vector.quantize_mx(
-                out=codes[:, 0 : m1 - m0].bitcast(FP8X4),
-                scales=y_sc[:, M * g + c0 : M * g + c1],
-                in_=y_b[(h, g, m0)][:, 0 : 4 * (m1 - m0)],
+                out=codes.bitcast(FP8X4),
+                scales=y_scale[:, M * g + first : M * g + last],
+                in_=y_grouped[h, g, cols.start],
             )
-            nc.sync.dma_start(out=out_words32[g, :, c0:c1], in_=codes[:, 0 : m1 - m0].bitcast(I32))
+            nc.sync.dma_start(out=out_words32[g, :, first:last], in_=codes.bitcast(I32))
 
         def store_scales(g):
             for q in range(4):
                 nc.sync.dma_start(
                     out=out_scales32[g, 4 * q : 4 * q + 4, :],
-                    in_=y_sc[32 * q : 32 * q + 4, M * g : M * (g + 1)].bitcast(I32),
+                    in_=y_scale[QUADRANT * q : QUADRANT * q + 4, M * g : M * (g + 1)].bitcast(I32),
                 )
 
-        nc.vector.memset(w_sraw[0][:].bitcast(I32), 0)
-        nc.vector.memset(x_sc[0][:].bitcast(I32), 0)
-        nc.vector.memset(sev_rows[:], 0.0)
-        nc.vector.memset(w_sraw[1][:].bitcast(I32), 0)
-        nc.vector.memset(x_sc[1][:].bitcast(I32), 0)
-        nc.gpsimd.dma_start(out=sev_raw[0:FP, :], in_=severity.rearrange("(j f) -> j f", j=FP))
+        on_vector = nc.vector.tensor_copy
+        on_scalar = nc.scalar.copy
+
+        nc.vector.memset(w_scale_raw[0][:].bitcast(I32), 0)
+        nc.vector.memset(x_scale[0][:].bitcast(I32), 0)
+        nc.vector.memset(w_scale_raw[1][:].bitcast(I32), 0)
+        nc.vector.memset(x_scale[1][:].bitcast(I32), 0)
+        nc.vector.memset(severity_rows[:], 0.0)
+        nc.gpsimd.dma_start(out=severity_raw[0:RISK_GROUPS, :], in_=severity.rearrange("(j f) -> j f", j=RISK_GROUPS))
         make_identity(nc, ident[:])
+        load_scales(nc.gpsimd, x_scale[1], x_scales32, 1)
+        for dst, src in zip(pair_in, (lower, upper, worth, burden)):
+            nc.gpsimd.dma_start(
+                out=dst[:].rearrange("p (g t) -> p g t", t=SLOTS),
+                in_=src.rearrange("(g p t) -> p g t", g=PAIR_GROUPS, t=SLOTS),
+            )
         load_w(0)
-        load_scales(w_sraw[0], w_scales32, 0)
+        load_scales(nc.sync, w_scale_raw[0], w_scales32, 0)
         load_x(0)
-        load_scales(x_sc[0], x_scales32, 0)
+        load_scales(nc.sync, x_scale[0], x_scales32, 0)
         load_w(1)
-        load_effect(e_first[0], 0, slice(0, G))
+        load_effect(effect_first[0], 0, whole)
         load_w(2)
-        load_scales(w_sraw[1], w_scales32, 1)
+        load_scales(nc.sync, w_scale_raw[1], w_scales32, 1)
         load_w(3)
-        load_effect(e_first[1], 1, slice(0, G))
-        load_effect(e_first[2], 2, slice(0, G))
+        load_effect(effect_first[1], 1, whole)
         load_x(1)
-        load_scales(x_sc[1], x_scales32, 1)
-        load_effect(e_first[3], 3, slice(0, G))
-        for v, src in enumerate((lower, upper, worth, burden)):
-            nc.sync.dma_start(out=vec[v][:], in_=src.rearrange("(g p t) -> p g t", g=NG, t=4))
-        for j in range(FP):
-            load_effect(e_rest[j], j, slice(G, N))
+        load_effect(effect_first[2], 2, whole)
+        load_effect(effect_first[3], 3, whole)
+        for j in risk_groups:
+            load_effect(effect_rest[j], j, slice(GROUP, N))
 
-        permute_w(0)
+        order_w(0)
         nc.vector.tensor_copy(
-            out=sev_rows[0:FP].rearrange("j t (b i) -> j t b i", i=4),
-            in_=sev_raw[0:FP, :].rearrange("j (b t i) -> j t b i", t=4, i=4),
+            out=severity_rows[0:RISK_GROUPS].rearrange("j t (b i) -> j t b i", i=RUN),
+            in_=severity_raw[0:RISK_GROUPS, :].rearrange("j (b t i) -> j t b i", t=SLOTS, i=RUN),
         )
-        stage1(0)
-        permute_w(1)
-        tag, sev_bank = take_bank()
-        for t in range(4):
-            nc.tensor.transpose(sev_bank[:, P * t : P * (t + 1)], sev_rows[:, t, :], ident[:])
-        stage1(1)
-        e_whole(0, "V")
-        nc.vector.tensor_copy(out=sev[:], in_=sev_bank[:].rearrange("p (t j) -> p j t", t=4)[:, 0:FP, :])
-        free_banks.append(tag)
-        permute_w(2)
-        stage1(2)
-        weigh(0)
-        permute_w(3)
-        stage1(3)
-        quant_whole(0)
-        quant_h(0)
-        e_whole(1, "V")
-        weigh(1)
-        quant_whole(1)
-        stage1(4)
-        quant_h(1)
-        e_whole(2, "V")
-        e_whole(3, "S")
-        weigh(2)
-        quant_whole(2)
-        stage1(5)
-        quant_h(2)
-        lo, hi, wo, bu = [vec[v][:].rearrange("p g t -> p (g t)") for v in range(4)]
-        nc.vector.tensor_copy(out=cst[:, 0, :], in_=wo)
-        nc.vector.tensor_scalar(out=cst[:, 1, :], in0=bu, scalar1=-1.0, scalar2=None, op0=ALU.mult)
-        nc.vector.tensor_tensor(out=cst[:, 4, :], in0=lo, in1=hi, op=ALU.min)
-        nc.vector.tensor_tensor(out=cst[:, 5, :], in0=hi, in1=wo, op=ALU.mult)
-        nc.vector.tensor_tensor(out=cst[:, 6, :], in0=cst[:, 4, :], in1=wo, op=ALU.mult)
-        nc.vector.tensor_tensor(out=cst[:, 7, :], in0=cst[:, 5, :], in1=bu, op=ALU.subtract)
-        nc.vector.tensor_tensor(out=cst[:, 4, :], in0=cst[:, 6, :], in1=bu, op=ALU.subtract)
-        nc.vector.tensor_tensor(out=cst[:, 2, :], in0=cst[:, 4, :], in1=cst[:, 7, :], op=ALU.min)
-        nc.vector.tensor_tensor(out=cst[:, 3, :], in0=cst[:, 4, :], in1=cst[:, 7, :], op=ALU.max)
+        risk_scores(0, 0)
+        order_w(1)
+        severity_tag, severity_bank = take_bank()
+        for t in range(SLOTS):
+            nc.tensor.transpose(severity_bank[:, P * t : P * (t + 1)], severity_rows[:, t, :], ident[:])
+        risk_scores(0, 1)
+        group_effect(0, 0, on_vector)
+        nc.vector.tensor_copy(
+            out=severity_col[:],
+            in_=severity_bank[:].rearrange("p (t j) -> p j t", t=SLOTS)[:, 0:RISK_GROUPS, :],
+        )
+        free_banks.append(severity_tag)
+        order_w(2)
+        risk_scores(0, 2)
+        weigh(0, 0)
+        order_w(3)
+        risk_scores(0, 3)
+        quantise_effect(0, 0)
+        quantise_h(0, 0)
 
-        weigh(3)
-        stage1(6)
-        stage1(7)
-        one_pass(0, 0, 0)
-        one_pass(0, 0, 1)
-        one_pass(0, 0, 2)
-        quant_whole(3)
-        quant_h(3)
-        one_pass(0, 0, 3)
-        e_whole(4, "V")
-        e_whole(6, "S")
-        finish(0, 0)
-        e_whole(5, "V")
-        quant_whole(4)
-        one_pass(0, 1, 0)
-        e_whole(7, "V")
-        quant_whole(5)
-        one_pass(0, 1, 1)
-        quant_whole(6)
-        one_pass(0, 1, 2)
-        quant_whole(7)
-        one_pass(0, 1, 3)
-        clamp(0, 0, range(4))
-        e_whole(8, "S")
-        finish(0, 1)
-        turn(0, 0, "SSSS")
-        weigh(4)
-        quant_whole(8)
-        quant_h(4)
-        one_pass(1, 0, 0)
-        y_group(0, 0, eng="S")
-        weigh(5)
-        clamp(0, 1, range(4))
-        quant_h(5)
-        turn(0, 1, "SSSS")
-        one_pass(1, 0, 1)
-        e_whole(9, "S")
-        weigh(6)
-        y_quant(0, 0)
-        quant_h(6)
-        one_pass(1, 0, 2)
-        one_pass(1, 1, 0)
-        one_pass(1, 1, 1)
-        one_pass(1, 1, 2)
-        e_whole(10, "S")
-        weigh(7)
-        quant_whole(9)
-        quant_h(7)
-        one_pass(1, 0, 3)
-        finish(1, 0)
-        one_pass(1, 1, 3)
-        e_whole(11, "V")
-        quant_whole(10)
-        quant_whole(11)
-        clamp(1, 0, range(4))
-        finish(1, 1)
-        stage2(0, 2, range(2))
-        turn(1, 0, "SSSS")
-        y_group(0, 1)
-        clamp(1, 1, range(4))
-        y_group(1, 0)
-        y_quant(0, 1)
-        stage2(0, 2, range(2, 4))
-        turn(1, 1, "SSSS")
-        y_quant(1, 0)
+        group_effect(1, 0, on_vector)
+        weigh(0, 1)
+        quantise_effect(1, 0)
+        risk_scores(1, 0)
+        quantise_h(0, 1)
+
+        group_effect(2, 0, on_vector)
+        group_effect(3, 0, on_scalar)
+        weigh(0, 2)
+        quantise_effect(2, 0)
+        risk_scores(1, 1)
+        quantise_h(0, 2)
+
+        lower_in, upper_in, worth_in, burden_in = [tile[:] for tile in pair_in]
+        nc.vector.tensor_copy(out=gain[:], in_=worth_in)
+        nc.vector.tensor_scalar(out=shift[:], in0=burden_in, scalar1=-1.0, scalar2=None, op0=ALU.mult)
+        nc.vector.tensor_tensor(out=least[:], in0=lower_in, in1=upper_in, op=ALU.min)
+        nc.vector.tensor_tensor(out=image_upper[:], in0=upper_in, in1=worth_in, op=ALU.mult)
+        nc.vector.tensor_tensor(out=image_least[:], in0=least[:], in1=worth_in, op=ALU.mult)
+        nc.vector.tensor_tensor(out=image_upper[:], in0=image_upper[:], in1=burden_in, op=ALU.subtract)
+        nc.vector.tensor_tensor(out=image_least[:], in0=image_least[:], in1=burden_in, op=ALU.subtract)
+        nc.vector.tensor_tensor(out=low[:], in0=image_least[:], in1=image_upper[:], op=ALU.min)
+        nc.vector.tensor_tensor(out=high[:], in0=image_least[:], in1=image_upper[:], op=ALU.max)
+
+        weigh(0, 3)
+        risk_scores(1, 2)
+        risk_scores(1, 3)
+        for j in range(RISK_GROUPS - 1):
+            block_pass(0, 0, j)
+        quantise_effect(3, 0)
+        quantise_h(0, 3)
+        block_pass(0, 0, 3)
+
+        group_effect(0, 1, on_vector)
+        group_effect(2, 1, on_scalar)
+        close_block(0, 0)
+        group_effect(1, 1, on_vector)
+        quantise_effect(0, 1)
+        block_pass(0, 1, 0)
+        group_effect(3, 1, on_vector)
+        for j in range(1, RISK_GROUPS):
+            quantise_effect(j, 1)
+            block_pass(0, 1, j)
+        bound(0, 0, whole)
+        group_effect(0, 2, on_scalar)
+        close_block(0, 1)
+        store_block(0, 0)
+
+        weigh(1, 0)
+        quantise_effect(0, 2)
+        quantise_h(1, 0)
+        block_pass(1, 0, 0)
+        group_y(0, 0, whole, on_scalar)
+        weigh(1, 1)
+        bound(0, 1, whole)
+        quantise_h(1, 1)
+        store_block(0, 1)
+        block_pass(1, 0, 1)
+        group_effect(1, 2, on_scalar)
+        weigh(1, 2)
+        quantise_h(1, 2)
+        block_pass(1, 0, 2)
+        for j in range(RISK_GROUPS - 1):
+            block_pass(1, 1, j)
+        group_effect(2, 2, on_scalar)
+        weigh(1, 3)
+        quantise_effect(1, 2)
+        quantise_h(1, 3)
+        block_pass(1, 0, 3)
+        close_block(1, 0)
+        block_pass(1, 1, 3)
+
+        group_effect(3, 2, on_vector)
+        quantise_effect(2, 2)
+        quantise_effect(3, 2)
+        bound(1, 0, whole)
+        quantise_y(0, 0, whole)
+        close_block(1, 1)
+        new_block(0, 2)
+        block_slots(0, 2, range(0, 2), whole)
+        store_block(1, 0)
+        group_y(0, 1, whole, on_vector)
+        bound(1, 1, whole)
+        group_y(1, 0, whole, on_vector)
+        quantise_y(0, 1, whole)
+        block_slots(0, 2, range(2, SLOTS), whole)
+        store_block(1, 1)
+        quantise_y(1, 0, whole)
         store_scales(0)
-        y_group(1, 1)
-        clamp(0, 2, range(4))
-        y_quant(1, 1)
+        group_y(1, 1, whole, on_vector)
+        bound(0, 2, whole)
+        quantise_y(1, 1, whole)
         store_scales(1)
-        half = G // 2
-        stage2(1, 2, range(4), 0, half)
-        turn(0, 2, "SSSS")
-        y_group(0, 2)
-        clamp(1, 2, range(4), 0, half)
-        y_quant(0, 2)
-        stage2(1, 2, range(4), half, G)
-        turn(1, 2, "SS")
-        y_group(1, 2, 0, half)
-        clamp(1, 2, range(4), half, G)
-        y_quant(1, 2, 0, half)
-        y_group(1, 2, half, G)
-        turn(1, 2, "SV", 2)
-        y_quant(1, 2, half, G)
+
+        front = slice(0, GROUP // 2)
+        back = slice(GROUP // 2, GROUP)
+        new_block(1, 2)
+        block_slots(1, 2, range(SLOTS), front)
+        store_block(0, 2)
+        group_y(0, 2, whole, on_vector)
+        bound(1, 2, front)
+        quantise_y(0, 2, whole)
+        block_slots(1, 2, range(SLOTS), back)
+        store_rows(1, 2, 0, on_scalar)
+        store_rows(1, 2, 1, on_scalar)
+        group_y(1, 2, front, on_vector)
+        bound(1, 2, back)
+        quantise_y(1, 2, front)
+        group_y(1, 2, back, on_vector)
+        store_rows(1, 2, 2, on_scalar)
+        store_rows(1, 2, 3, on_vector)
+        quantise_y(1, 2, back)
         store_scales(2)

@@ -109,10 +109,10 @@ def tile_clipped_treatment_utility_h2_kernel(
                 in_=x_words32[:, :, GROUP * h : GROUP * (h + 1)].rearrange("c p w -> p c w"),
             )
 
-        def load_scales(queue, plane, rows32, half):
+        def load_scales(plane, rows32, half):
             words = rows32.shape[2] // 2
             for q in range(4):
-                queue.dma_start(
+                nc.sync.dma_start(
                     out=plane[QUADRANT * q : QUADRANT * q + 4, :].bitcast(I32).rearrange("r (c w) -> r c w", c=LAB_GROUPS),
                     in_=rows32[:, 4 * q : 4 * q + 4, words * half : words * (half + 1)].rearrange("c r w -> r c w"),
                 )
@@ -295,25 +295,25 @@ def tile_clipped_treatment_utility_h2_kernel(
         nc.vector.memset(severity_rows[:], 0.0)
         nc.gpsimd.dma_start(out=severity_raw[0:RISK_GROUPS, :], in_=severity.rearrange("(j f) -> j f", j=RISK_GROUPS))
         make_identity(nc, ident[:])
-        load_scales(nc.gpsimd, x_scale[1], x_scales32, 1)
-        for dst, src in zip(pair_in, (lower, upper, worth, burden)):
-            nc.gpsimd.dma_start(
-                out=dst[:].rearrange("p (g t) -> p g t", t=SLOTS),
-                in_=src.rearrange("(g p t) -> p g t", g=PAIR_GROUPS, t=SLOTS),
-            )
         load_w(0)
-        load_scales(nc.sync, w_scale_raw[0], w_scales32, 0)
+        load_scales(w_scale_raw[0], w_scales32, 0)
         load_x(0)
-        load_scales(nc.sync, x_scale[0], x_scales32, 0)
+        load_scales(x_scale[0], x_scales32, 0)
         load_w(1)
         load_effect(effect_first[0], 0, whole)
         load_w(2)
-        load_scales(nc.sync, w_scale_raw[1], w_scales32, 1)
+        load_scales(w_scale_raw[1], w_scales32, 1)
         load_w(3)
         load_effect(effect_first[1], 1, whole)
         load_x(1)
+        load_scales(x_scale[1], x_scales32, 1)
         load_effect(effect_first[2], 2, whole)
         load_effect(effect_first[3], 3, whole)
+        for dst, src in zip(pair_in, (lower, upper, worth, burden)):
+            nc.sync.dma_start(
+                out=dst[:].rearrange("p (g t) -> p g t", t=SLOTS),
+                in_=src.rearrange("(g p t) -> p g t", g=PAIR_GROUPS, t=SLOTS),
+            )
         for j in risk_groups:
             load_effect(effect_rest[j], j, slice(GROUP, N))
 

from contextlib import ExitStack

import concourse.mybir as mybir
from concourse.masks import make_identity

M, K, F, N = 1024, 1024, 2048, 1536
FLOPS = 2 * M * K * F + 2 * M * F * N

F32 = mybir.dt.float32
BF16 = mybir.dt.bfloat16
I32 = mybir.dt.int32
U32 = mybir.dt.uint32
U8 = mybir.dt.uint8
FP8X4 = mybir.dt.float8_e4m3fn_x4
FP4X4 = mybir.dt.float4_e2m1fn_x4
ACT = mybir.ActivationFunctionType
ALU = mybir.AluOpType

P = 128
SLOTS = 4
GROUP = P * SLOTS
LAB_GROUPS = K // GROUP
RISK_GROUPS = F // GROUP
PAIR_GROUPS = N // GROUP
HALVES = M // GROUP
BANKS = 8
QUADRANT = 32
RUN = 4
W_BYTES = 2 * GROUP
X_BYTES = 4 * GROUP

SMALL_SLOTS = 13
LARGE_SLOTS = 8
SIGMOID_SLOTS = 4
BLOCK_SLOTS = 4


def tile_clipped_treatment_utility_h2_kernel(
    tc, x_words, x_scales, w_words, w_scales, severity, effect, lower, upper, worth, burden, out_0, out_1, out_2
):
    nc = tc.nc
    with ExitStack() as ctx:
        keep = ctx.enter_context(tc.tile_pool(name="keep", bufs=1))
        work = ctx.enter_context(tc.tile_pool(name="work", bufs=1))
        psum = ctx.enter_context(tc.psum_pool(name="psum", bufs=1))
        ctx.enter_context(tc.manual_schedule())

        def kept(name, shape, dtype):
            return keep.tile(shape, dtype, name=name, align_bytes=64)

        def small(name, shape, dtype):
            return work.tile(shape, dtype, name=name, tag="small", bufs=SMALL_SLOTS, align_bytes=64)

        def large(name, shape, dtype):
            return work.tile(shape, dtype, name=name, tag="large", bufs=LARGE_SLOTS, align_bytes=64)

        risk_groups = range(RISK_GROUPS)
        pieces = [(j, g) for g in range(PAIR_GROUPS) for j in risk_groups]
        h_parts = [(h, j) for h in range(HALVES) for j in risk_groups]

        w_raw = [small("w_raw", [P, LAB_GROUPS * W_BYTES], U8) for j in risk_groups]
        w_codes = [kept("w_codes%d" % j, [P, LAB_GROUPS * W_BYTES], U8) for j in risk_groups]
        w_scale_raw = [kept("w_scale_raw%d" % a, [P, LAB_GROUPS * F // 2], U8) for a in range(2)]
        w_scale = [kept("w_scale%d" % j, [P, LAB_GROUPS * GROUP], U8) for j in risk_groups]
        x_scale = [kept("x_scale%d" % h, [P, LAB_GROUPS * GROUP], U8) for h in range(HALVES)]
        effect_first = [large("effect_first", [P, SLOTS, GROUP], BF16) for j in risk_groups]
        x_codes = [large("x_codes", [P, LAB_GROUPS * X_BYTES], U8) for h in range(HALVES)]
        effect_rest = [kept("effect_rest%d" % j, [P, SLOTS, N - GROUP], BF16) for j in risk_groups]
        e_codes = {(j, g): kept("e_codes%d_%d" % (j, g), [P, GROUP], U32) for j, g in pieces}
        e_scale = {(j, g): kept("e_scale%d_%d" % (j, g), [P, GROUP], U8) for j, g in pieces}
        h_codes = {(h, j): kept("h_codes%d_%d" % (h, j), [P, GROUP], U32) for h, j in h_parts}
        h_scale = {(h, j): kept("h_scale%d_%d" % (h, j), [P, GROUP], U8) for h, j in h_parts}
        h_grouped = [kept("h_grouped%d" % b, [P, SLOTS * GROUP], BF16) for b in range(2)]
        y_scale = kept("y_scale", [P, PAIR_GROUPS * M], U8)
        ident = kept("ident", [P, P], F32)
        severity_raw = kept("severity_raw", [P, GROUP], BF16)
        severity_rows = small("severity_rows", [P, SLOTS, P], F32)
        severity_col = kept("severity_col", [P, RISK_GROUPS, SLOTS], F32)
        pair_cols = PAIR_GROUPS * SLOTS
        pair_in = [kept("pair_in%d" % v, [P, pair_cols], BF16) for v in range(4)]
        gain, shift, low, high, least, image_least, image_upper = [
            kept(name, [P, pair_cols], F32)
            for name in ("gain", "shift", "low", "high", "least", "image_least", "image_upper")
        ]

        w_words32 = w_words.bitcast(I32)
        w_scales32 = w_scales.bitcast(I32)
        x_words32 = x_words.rearrange("c p m t -> c p (m t)").bitcast(I32)
        x_scales32 = x_scales.bitcast(I32)
        out_words32 = out_1.rearrange("g p m t -> g p (m t)").bitcast(I32)
        out_scales32 = out_2.bitcast(I32)

        free_banks = ["bank%d" % b for b in range(BANKS)]

        def take_bank():
            tag = free_banks.pop(0)
            return tag, psum.tile([P, GROUP], F32, name=tag)

        def load_w(j):
            words = W_BYTES // 4
            nc.sync.dma_start(
                out=w_raw[j][:].bitcast(I32).rearrange("p (c w) -> p c w", c=LAB_GROUPS),
                in_=w_words32[:, :, words * j : words * (j + 1)].rearrange("c p w -> p c w"),
            )

        def load_x(h):
            nc.sync.dma_start(
                out=x_codes[h][:].bitcast(I32).rearrange("p (c w) -> p c w", c=LAB_GROUPS),
                in_=x_words32[:, :, GROUP * h : GROUP * (h + 1)].rearrange("c p w -> p c w"),
            )

        def load_scales(plane, rows32, half):
            words = rows32.shape[2] // 2
            for q in range(4):
                nc.sync.dma_start(
                    out=plane[QUADRANT * q : QUADRANT * q + 4, :].bitcast(I32).rearrange("r (c w) -> r c w", c=LAB_GROUPS),
                    in_=rows32[:, 4 * q : 4 * q + 4, words * half : words * (half + 1)].rearrange("c r w -> r c w"),
                )

        def load_effect(dst, j, cols):
            rows = effect[GROUP * j : GROUP * (j + 1), cols].rearrange("(b t i) n -> i b t n", t=SLOTS, i=RUN)
            for i in range(RUN):
                nc.sync.dma_start(out=dst[i:P:RUN, :, :], in_=rows[i])

        def order_w(j):
            nc.vector.tensor_copy(
                out=w_codes[j][:].bitcast(I32).rearrange("p (c t b w) -> p c t b w", c=LAB_GROUPS, t=SLOTS, w=2),
                in_=w_raw[j][:].bitcast(I32).rearrange("p (c b t w) -> p c t b w", c=LAB_GROUPS, t=SLOTS, w=2),
            )
            raw = w_scale_raw[j // 2][:].bitcast(I32)
            nc.vector.tensor_copy(
                out=w_scale[j][:].bitcast(I32).rearrange("p (c t b) -> p c t b", c=LAB_GROUPS, t=SLOTS),
                in_=raw.rearrange("p (c j b t) -> p j c t b", c=LAB_GROUPS, j=2, t=SLOTS)[:, j % 2],
            )

        scores = {}

        def risk_scores(h, j):
            scores[h, j] = work.tile([P, SLOTS, GROUP], F32, name="scores", bufs=SIGMOID_SLOTS)
            for t in range(SLOTS):
                tag, bank = take_bank()
                for c in range(LAB_GROUPS):
                    col = GROUP * c + P * t
                    nc.tensor.matmul_mx(
                        out=bank[:],
                        lhsT=w_codes[j][:, 2 * col : 2 * (col + P)].bitcast(FP4X4),
                        lhsT_scale=w_scale[j][:, col : col + P],
                        rhs=x_codes[h][:, X_BYTES * c : X_BYTES * (c + 1)].bitcast(FP8X4),
                        rhs_scale=x_scale[h][:, GROUP * c : GROUP * (c + 1)],
                        start=(c == 0),
                        stop=(c == LAB_GROUPS - 1),
                    )
                nc.scalar.activation(out=scores[h, j][:, t, :], in_=bank[:], func=ACT.Sigmoid)
                free_banks.append(tag)

        def weigh(h, j):
            nc.vector.tensor_tensor(
                out=h_grouped[j % 2][:].rearrange("p (a i t) -> p a t i", i=2, t=SLOTS),
                in0=scores[h, j][:].rearrange("p t (a i) -> p a t i", i=2),
                in1=severity_col[:, j, :].unsqueeze(1).unsqueeze(3).broadcast_to([P, GROUP // 2, SLOTS, 2]),
                op=ALU.mult,
            )

        def quantise_h(h, j):
            nc.vector.quantize_mx(out=h_codes[h, j][:].bitcast(FP8X4), scales=h_scale[h, j][:], in_=h_grouped[j % 2][:])

        e_grouped = {}

        def group_effect(j, g, move):
            raw = effect_first[j][:] if g == 0 else effect_rest[j][:, :, GROUP * (g - 1) : GROUP * g]
            e_grouped[j, g] = large("grouped", [P, SLOTS * GROUP], BF16)
            move(
                out=e_grouped[j, g][:].rearrange("p (u a i t) -> p a u i t", u=SLOTS, i=2, t=SLOTS),
                in_=raw.rearrange("p t (a i u) -> p a u i t", i=2, u=SLOTS),
            )

        def quantise_effect(j, g):
            nc.vector.quantize_mx(out=e_codes[j, g][:].bitcast(FP8X4), scales=e_scale[j, g][:], in_=e_grouped[j, g][:])

        y_t = {}

        def new_block(h, g):
            y_t[h, g] = work.tile([P, SLOTS, GROUP], F32, name="y_t", bufs=BLOCK_SLOTS)

        def effect_pass(bank, h, g, t, j, cols):
            nc.tensor.matmul_mx(
                out=bank[:, cols],
                lhsT=e_codes[j, g][:, P * t : P * (t + 1)].bitcast(FP8X4),
                lhsT_scale=e_scale[j, g][:, P * t : P * (t + 1)],
                rhs=h_codes[h, j][:, cols].bitcast(FP8X4),
                rhs_scale=h_scale[h, j][:, cols],
                start=(j == 0),
                stop=(j == RISK_GROUPS - 1),
            )

        def empty_bank(tag, bank, h, g, t, cols):
            col = SLOTS * g + t
            nc.scalar.activation(
                out=y_t[h, g][:, t, cols],
                in_=bank[:, cols],
                func=ACT.Identity,
                scale=gain[:, col : col + 1],
                bias=shift[:, col : col + 1],
            )
            free_banks.append(tag)

        whole = slice(0, GROUP)
        open_banks = {}

        def block_pass(h, g, j):
            if j == 0:
                new_block(h, g)
            for t in range(SLOTS):
                if j == 0:
                    open_banks[h, g, t] = take_bank()
                effect_pass(open_banks[h, g, t][1], h, g, t, j, whole)

        def close_block(h, g):
            for t in range(SLOTS):
                empty_bank(*open_banks[h, g, t], h, g, t, whole)

        def block_slots(h, g, slots, cols):
            for t in slots:
                tag, bank = take_bank()
                for j in risk_groups:
                    effect_pass(bank, h, g, t, j, cols)
                empty_bank(tag, bank, h, g, t, cols)

        def bound(h, g, cols):
            for t in range(SLOTS):
                col = SLOTS * g + t
                nc.vector.tensor_scalar(
                    out=y_t[h, g][:, t, cols],
                    in0=y_t[h, g][:, t, cols],
                    scalar1=low[:, col : col + 1],
                    scalar2=high[:, col : col + 1],
                    op0=ALU.max,
                    op1=ALU.min,
                )

        def store_rows(h, g, tile_index, move):
            tag, bank = take_bank()
            first = P * tile_index
            for t in range(SLOTS):
                nc.tensor.transpose(bank[:, P * t : P * (t + 1)], y_t[h, g][:, t, first : first + P], ident[:])
            rows = small("rows", [P, GROUP], F32)
            move(
                out=rows[:].rearrange("m (p t) -> m p t", t=SLOTS),
                in_=bank[:].rearrange("m (t p) -> m p t", t=SLOTS),
            )
            free_banks.append(tag)
            row = GROUP * h + first
            nc.sync.dma_start(out=out_0[row : row + P, GROUP * g : GROUP * (g + 1)], in_=rows[:])

        def store_block(h, g):
            for tile_index in range(GROUP // P):
                store_rows(h, g, tile_index, on_scalar)

        y_grouped = {}

        def group_y(h, g, cols, move):
            width = SLOTS * (cols.stop - cols.start)
            staged = large("grouped", [P, SLOTS * GROUP], BF16)
            y_grouped[h, g, cols.start] = staged[:, 0:width]
            move(
                out=staged[:, 0:width].rearrange("p (a i t) -> p a t i", i=4, t=SLOTS),
                in_=y_t[h, g][:, :, cols].rearrange("p t (a i) -> p a t i", i=4),
            )

        def quantise_y(h, g, cols):
            codes = small("y_codes", [P, GROUP], U32)[:, 0 : cols.stop - cols.start]
            first = GROUP * h + cols.start
            last = GROUP * h + cols.stop
            nc.vector.quantize_mx(
                out=codes.bitcast(FP8X4),
                scales=y_scale[:, M * g + first : M * g + last],
                in_=y_grouped[h, g, cols.start],
            )
            nc.sync.dma_start(out=out_words32[g, :, first:last], in_=codes.bitcast(I32))

        def store_scales(g):
            for q in range(4):
                nc.sync.dma_start(
                    out=out_scales32[g, 4 * q : 4 * q + 4, :],
                    in_=y_scale[QUADRANT * q : QUADRANT * q + 4, M * g : M * (g + 1)].bitcast(I32),
                )

        on_vector = nc.vector.tensor_copy
        on_scalar = nc.scalar.copy

        nc.vector.memset(w_scale_raw[0][:].bitcast(I32), 0)
        nc.vector.memset(x_scale[0][:].bitcast(I32), 0)
        nc.vector.memset(w_scale_raw[1][:].bitcast(I32), 0)
        nc.vector.memset(x_scale[1][:].bitcast(I32), 0)
        nc.vector.memset(severity_rows[:], 0.0)
        nc.gpsimd.dma_start(out=severity_raw[0:RISK_GROUPS, :], in_=severity.rearrange("(j f) -> j f", j=RISK_GROUPS))
        make_identity(nc, ident[:])
        load_w(0)
        load_scales(w_scale_raw[0], w_scales32, 0)
        load_x(0)
        load_scales(x_scale[0], x_scales32, 0)
        load_w(1)
        load_effect(effect_first[0], 0, whole)
        load_w(2)
        load_scales(w_scale_raw[1], w_scales32, 1)
        load_w(3)
        load_effect(effect_first[1], 1, whole)
        load_x(1)
        load_scales(x_scale[1], x_scales32, 1)
        load_effect(effect_first[2], 2, whole)
        load_effect(effect_first[3], 3, whole)
        for dst, src in zip(pair_in, (lower, upper, worth, burden)):
            nc.sync.dma_start(
                out=dst[:].rearrange("p (g t) -> p g t", t=SLOTS),
                in_=src.rearrange("(g p t) -> p g t", g=PAIR_GROUPS, t=SLOTS),
            )
        for j in risk_groups:
            load_effect(effect_rest[j], j, slice(GROUP, N))

        order_w(0)
        nc.vector.tensor_copy(
            out=severity_rows[0:RISK_GROUPS].rearrange("j t (b i) -> j t b i", i=RUN),
            in_=severity_raw[0:RISK_GROUPS, :].rearrange("j (b t i) -> j t b i", t=SLOTS, i=RUN),
        )
        risk_scores(0, 0)
        order_w(1)
        severity_tag, severity_bank = take_bank()
        for t in range(SLOTS):
            nc.tensor.transpose(severity_bank[:, P * t : P * (t + 1)], severity_rows[:, t, :], ident[:])
        risk_scores(0, 1)
        group_effect(0, 0, on_vector)
        nc.vector.tensor_copy(
            out=severity_col[:],
            in_=severity_bank[:].rearrange("p (t j) -> p j t", t=SLOTS)[:, 0:RISK_GROUPS, :],
        )
        free_banks.append(severity_tag)
        order_w(2)
        risk_scores(0, 2)
        weigh(0, 0)
        order_w(3)
        risk_scores(0, 3)
        quantise_effect(0, 0)
        quantise_h(0, 0)

        group_effect(1, 0, on_vector)
        weigh(0, 1)
        quantise_effect(1, 0)
        risk_scores(1, 0)
        quantise_h(0, 1)

        group_effect(2, 0, on_vector)
        group_effect(3, 0, on_scalar)
        weigh(0, 2)
        quantise_effect(2, 0)
        risk_scores(1, 1)
        quantise_h(0, 2)

        lower_in, upper_in, worth_in, burden_in = [tile[:] for tile in pair_in]
        nc.vector.tensor_copy(out=gain[:], in_=worth_in)
        nc.vector.tensor_scalar(out=shift[:], in0=burden_in, scalar1=-1.0, scalar2=None, op0=ALU.mult)
        nc.vector.tensor_tensor(out=least[:], in0=lower_in, in1=upper_in, op=ALU.min)
        nc.vector.tensor_tensor(out=image_upper[:], in0=upper_in, in1=worth_in, op=ALU.mult)
        nc.vector.tensor_tensor(out=image_least[:], in0=least[:], in1=worth_in, op=ALU.mult)
        nc.vector.tensor_tensor(out=image_upper[:], in0=image_upper[:], in1=burden_in, op=ALU.subtract)
        nc.vector.tensor_tensor(out=image_least[:], in0=image_least[:], in1=burden_in, op=ALU.subtract)
        nc.vector.tensor_tensor(out=low[:], in0=image_least[:], in1=image_upper[:], op=ALU.min)
        nc.vector.tensor_tensor(out=high[:], in0=image_least[:], in1=image_upper[:], op=ALU.max)

        weigh(0, 3)
        risk_scores(1, 2)
        risk_scores(1, 3)
        for j in range(RISK_GROUPS - 1):
            block_pass(0, 0, j)
        quantise_effect(3, 0)
        quantise_h(0, 3)
        block_pass(0, 0, 3)

        group_effect(0, 1, on_vector)
        group_effect(2, 1, on_scalar)
        close_block(0, 0)
        group_effect(1, 1, on_vector)
        quantise_effect(0, 1)
        block_pass(0, 1, 0)
        group_effect(3, 1, on_vector)
        for j in range(1, RISK_GROUPS):
            quantise_effect(j, 1)
            block_pass(0, 1, j)
        bound(0, 0, whole)
        group_effect(0, 2, on_scalar)
        close_block(0, 1)
        store_block(0, 0)

        weigh(1, 0)
        quantise_effect(0, 2)
        quantise_h(1, 0)
        block_pass(1, 0, 0)
        group_y(0, 0, whole, on_scalar)
        weigh(1, 1)
        bound(0, 1, whole)
        quantise_h(1, 1)
        store_block(0, 1)
        block_pass(1, 0, 1)
        group_effect(1, 2, on_scalar)
        weigh(1, 2)
        quantise_h(1, 2)
        block_pass(1, 0, 2)
        for j in range(RISK_GROUPS - 1):
            block_pass(1, 1, j)
        group_effect(2, 2, on_scalar)
        weigh(1, 3)
        quantise_effect(1, 2)
        quantise_h(1, 3)
        block_pass(1, 0, 3)
        close_block(1, 0)
        block_pass(1, 1, 3)

        group_effect(3, 2, on_vector)
        quantise_effect(2, 2)
        quantise_effect(3, 2)
        bound(1, 0, whole)
        quantise_y(0, 0, whole)
        close_block(1, 1)
        new_block(0, 2)
        block_slots(0, 2, range(0, 2), whole)
        store_block(1, 0)
        group_y(0, 1, whole, on_vector)
        bound(1, 1, whole)
        group_y(1, 0, whole, on_vector)
        quantise_y(0, 1, whole)
        block_slots(0, 2, range(2, SLOTS), whole)
        store_block(1, 1)
        quantise_y(1, 0, whole)
        store_scales(0)
        group_y(1, 1, whole, on_vector)
        bound(0, 2, whole)
        quantise_y(1, 1, whole)
        store_scales(1)

        front = slice(0, GROUP // 2)
        back = slice(GROUP // 2, GROUP)
        new_block(1, 2)
        block_slots(1, 2, range(SLOTS), front)
        store_block(0, 2)
        group_y(0, 2, whole, on_vector)
        bound(1, 2, front)
        quantise_y(0, 2, whole)
        block_slots(1, 2, range(SLOTS), back)
        store_rows(1, 2, 0, on_scalar)
        store_rows(1, 2, 1, on_scalar)
        group_y(1, 2, front, on_vector)
        bound(1, 2, back)
        quantise_y(1, 2, front)
        group_y(1, 2, back, on_vector)
        store_rows(1, 2, 2, on_scalar)
        store_rows(1, 2, 3, on_vector)
        quantise_y(1, 2, back)
        store_scales(2)
